import numpy as np
import ml_dtypes


def mxq(x, axis, fmt="e4m3"):
    dtype, down = {"e4m3": (ml_dtypes.float8_e4m3fn, 7), "e5m2": (ml_dtypes.float8_e5m2, 14)}[fmt]
    v = np.moveaxis(np.asarray(x, np.float32).astype(ml_dtypes.bfloat16).astype(np.float64), axis, -1)
    blocks = v.reshape(v.shape[:-1] + (-1, 32))
    amax = np.abs(blocks).max(-1, keepdims=True)
    byte = np.maximum(np.where(amax > 0, np.frexp(amax)[1] - 1 + 127, 0) - down, 1)
    scale = np.exp2(byte - 127.0)
    codes = (blocks / scale).astype(np.float32).astype(dtype).astype(np.float64)
    return np.moveaxis((codes * scale).reshape(v.shape), -1, axis)


WIDE = False


def mx_kscale(k):
    if not WIDE:
        return np.ones(k)
    levels = np.array([10, -10, 5, -5, 0])
    if k % 512:
        return np.exp2(np.random.permutation(np.resize(levels, k // 32))).repeat(32)
    a = np.empty((k // 512, 16))
    for p in range(k // 512):
        a[p, :8] = np.random.permutation(np.resize(levels, 8))
        for g in range(8):
            far = levels[np.abs(levels - a[p, g]) >= 10]
            a[p, g + 8] = far[np.random.randint(len(far))]
    return np.exp2(a.ravel()).repeat(32)


BF16 = ml_dtypes.bfloat16


def bf(x):
    return np.asarray(x, np.float32).astype(BF16)


def f64(x):
    return np.asarray(x).astype(np.float64)


E2M1 = np.array([0.0, 0.5, 1.0, 1.5, 2.0, 3.0, 4.0, 6.0, -0.0, -0.5, -1.0, -1.5, -2.0, -3.0, -4.0, -6.0])


def pack_weight(w, fmt):
    k, n = w.shape
    w = f64(bf(w)).reshape(k // 32, 32, n)
    amax = np.abs(w).max(1)
    if fmt == "e4m3":
        byte = np.frexp(amax)[1] - 1 + 127 - 7
    else:
        mant, ex = np.frexp(amax / 6.0)
        byte = np.where(mant > 0.5, ex, ex - 1) + 127
    byte = np.clip(np.where(amax > 0, byte, 1), 1, 254)
    scaled = (w * np.exp2(127.0 - byte)[:, None, :]).reshape(k, n).astype(np.float32)
    by_word = np.ascontiguousarray(scaled.reshape(k // 512, 128, 4, n).transpose(0, 1, 3, 2))
    if fmt == "e4m3":
        words = by_word.astype(ml_dtypes.float8_e4m3fn).view(np.uint8)
    else:
        c = by_word.astype(ml_dtypes.float4_e2m1fn).view(np.uint8) & 0xF
        words = c[..., 0::2] | (c[..., 1::2] << 4)
    return np.ascontiguousarray(words), np.ascontiguousarray(byte.astype(np.uint8).reshape(k // 512, 16, n))


def unpack_weight(words, scales, fmt):
    g, p, n, _ = words.shape
    if fmt == "e4m3":
        vals = np.ascontiguousarray(words).view(ml_dtypes.float8_e4m3fn).astype(np.float64)
    else:
        nib = np.empty((g, p, n, 4), np.uint8)
        nib[..., 0::2] = words & 0xF
        nib[..., 1::2] = words >> 4
        vals = E2M1[nib]
    vals = vals * np.repeat(np.exp2(scales.astype(np.float64) - 127.0), 8, axis=1)[..., None]
    return vals.transpose(0, 1, 3, 2).reshape(g * 512, n)
def pack4(w):
    words, scales = pack_weight(w, "e2m1")
    return words.reshape(words.shape[0], 128, -1), scales


def unpack4(words, scales):
    return unpack_weight(words.reshape(words.shape[0], 128, -1, 2), scales, "e2m1")


T, D, C, N = 2048, 1536, 512, 1024

W_LOW, W_HIGH = -0.5, 1.0


def setup_inputs():
    s = mx_kscale(D)
    r = mx_kscale(C)
    skin_solver = 0.5 * np.random.standard_normal((D, N)) / np.sqrt(D)
    skin_words, skin_scales = pack4(skin_solver / s[:, None])
    return {"skin": bf(np.random.standard_normal((T, D)) * s),
            "skin_words": skin_words,
            "skin_scales": skin_scales,
            "lips": bf(np.random.standard_normal((T, C)) * r),
            "lip_solver": bf(0.5 * np.random.standard_normal((C, N)) / np.sqrt(C) / r[:, None]),
            "actor_bias": bf(0.2 * np.random.standard_normal(N)),
            "travel": bf(1 + 0.1 * np.random.standard_normal(N)),
            "rest": bf(0.3 * np.random.standard_normal(N))}


def reference(skin, skin_words, skin_scales, lips, lip_solver, actor_bias, travel, rest):
    from_skin = mxq(f64(skin), 1, "e4m3") @ unpack4(skin_words, skin_scales)
    from_lips = mxq(f64(lips), 1, "e4m3") @ mxq(f64(lip_solver), 0, "e4m3")
    raw = from_skin + from_lips + f64(actor_bias)
    weights = np.minimum(np.maximum(raw, W_LOW), W_HIGH)
    return f64(rest) + f64(travel) * weights

@@ -1,0 +1,399 @@
+from contextlib import ExitStack
+
+import concourse.mybir as mybir
+from concourse.masks import make_identity
+
+T, D, C, N = 2048, 1536, 512, 1024
+FLOPS = 2 * T * (D + C) * N
+
+F32 = mybir.dt.float32
+BF16 = mybir.dt.bfloat16
+I32 = mybir.dt.int32
+U32 = mybir.dt.uint32
+U8 = mybir.dt.uint8
+FP8X4 = mybir.dt.float8_e4m3fn_x4
+FP4X4 = mybir.dt.float4_e2m1fn_x4
+ALU = mybir.AluOpType
+ACT = mybir.ActivationFunctionType
+
+P = 128
+KP = 512
+SKIN_PASSES = D // KP
+PASSES = SKIN_PASSES + 1
+GROUP = 512
+TILES = GROUP // P
+HALF = 512
+BLOCKS = HALF // P
+W_LOW, W_HIGH = -0.5, 1.0
+
+
+def tile_face_retarget_rig_s1_kernel(
+    tc, skin, skin_words, skin_scales, lips, lip_solver, actor_bias, travel, rest, out
+):
+    nc = tc.nc
+    with ExitStack() as ctx:
+        keep = ctx.enter_context(tc.tile_pool(name="keep", bufs=1))
+        work = ctx.enter_context(tc.tile_pool(name="work", bufs=3))
+        psum = ctx.enter_context(tc.psum_pool(name="psum", bufs=1))
+
+        skin_sc = keep.tile([P, SKIN_PASSES * N], U8, align_bytes=64)
+        vec_rows = keep.tile([P, P], BF16, align_bytes=64)
+        ident = keep.tile([P, P], F32, align_bytes=64)
+        warm = keep.tile([P, 1], F32)
+        nc.vector.memset(vec_rows[:], 0.0)
+        nc.vector.memset(skin_sc[:].bitcast(I32), 0)
+        nc.vector.memset(warm[:], 0.0)
+        make_identity(nc, ident[:])
+        nc.scalar.activation(out=warm[:], in_=warm[:], func=ACT.Relu)
+
+        for v, vec in enumerate((actor_bias, travel, rest)):
+            nc.sync.dma_start(out=vec_rows[8 * v : 8 * v + 8, :], in_=vec.rearrange("(c p) -> c p", p=P))
+
+        words = [keep.tile([P, SKIN_PASSES, 2 * HALF], U8, name=f"words{h}", align_bytes=64) for h in range(2)]
+        solver_raw = [keep.tile([P, 4, HALF], BF16, name=f"solver_raw{h}", align_bytes=64) for h in range(2)]
+        solver_grp = [keep.tile([P, HALF, 4], BF16, name=f"solver_grp{h}", align_bytes=64) for h in range(2)]
+        solver_codes = [keep.tile([P, HALF], U32, name=f"solver_codes{h}", align_bytes=64) for h in range(2)]
+        solver_sc = [keep.tile([P, HALF], U8, name=f"solver_sc{h}", align_bytes=64) for h in range(2)]
+        codes = [keep.tile([P, PASSES, GROUP], U32, name=f"codes{g}", align_bytes=64) for g in range(4)]
+        scales = [keep.tile([P, PASSES, GROUP], U8, name=f"scales{g}", align_bytes=64) for g in range(4)]
+        head_raw = [keep.tile([P, D + C], BF16, name=f"head_raw{j}", align_bytes=64) for j in range(TILES)]
+        raw = {
+            (g, c): keep.tile([P, TILES, KP], BF16, name=f"raw{g}_{c}", align_bytes=64)
+            for g in range(1, 4)
+            for c in range(PASSES)
+        }
+
+        def group_rows(x, g):
+            return x[GROUP * g : GROUP * (g + 1), :].rearrange("(p j) k -> p j k", j=TILES)
+
+        def load_head(j):
+            nc.sync.dma_start(out=head_raw[j][:, 0:D], in_=group_rows(skin, 0)[:, j, :])
+            nc.sync.dma_start(out=head_raw[j][:, D : D + C], in_=group_rows(lips, 0)[:, j, :])
+
+        def load_words(h):
+            nc.sync.dma_start(
+                out=words[h][:],
+                in_=skin_words.rearrange("g p n -> p g n")[:, :, 2 * HALF * h : 2 * HALF * (h + 1)],
+            )
+
+        def load_scales():
+            dst = skin_sc[:].bitcast(I32).rearrange("p (g n) -> p g n", g=SKIN_PASSES)
+            src = skin_scales.bitcast(I32)
+            for q in range(4):
+                nc.sync.dma_start(
+                    out=dst[32 * q : 32 * q + 4, :, :],
+                    in_=src[:, 4 * q : 4 * q + 4, :].rearrange("g r n -> r g n"),
+                )
+
+        def load_solver(h):
+            nc.sync.dma_start(
+                out=solver_raw[h][:],
+                in_=lip_solver.rearrange("(p j) n -> p j n", j=4)[:, :, HALF * h : HALF * (h + 1)],
+            )
+
+        load_head(0)
+        load_scales()
+        load_solver(0)
+        load_words(0)
+        load_head(1)
+        load_solver(1)
+        load_head(2)
+        load_head(3)
+        load_words(1)
+        for g in range(1, 4):
+            for c in range(PASSES):
+                src = group_rows(skin, g)[:, :, KP * c : KP * (c + 1)] if c < SKIN_PASSES else group_rows(lips, g)
+                nc.sync.dma_start(out=raw[g, c][:], in_=src)
+
+        vec_f32 = keep.tile([P, P], F32, align_bytes=64)
+        cols = keep.tile([P, 24], F32, align_bytes=64)
+        bias_up = keep.tile([P, 8], F32)
+        rest_low = keep.tile([P, 8], F32)
+        rest_high = keep.tile([P, 8], F32)
+        shift = keep.tile([P, 8], F32)
+        low = keep.tile([P, 8], F32)
+        high = keep.tile([P, 8], F32)
+        bias_row = keep.tile([P, HALF], F32, align_bytes=64)
+        travel_row = keep.tile([P, HALF], F32, align_bytes=64)
+        rest_row = keep.tile([P, HALF], F32, align_bytes=64)
+        b_col, t_col, r_col = cols[:, 0:8], cols[:, 8:16], cols[:, 16:24]
+
+        def vectors_to_columns():
+            nc.vector.tensor_copy(out=vec_f32[:], in_=vec_rows[:])
+            bank = psum.tile([P, 512], F32, name="vec_bank", tag="back", bufs=BACK)
+            nc.tensor.transpose(bank[:, 0:P], vec_f32[:], ident[:])
+            nc.vector.tensor_copy(out=cols[:], in_=bank[:, 0:24])
+            nc.vector.tensor_scalar(out=bias_up[:], in0=b_col, scalar1=-W_LOW, scalar2=None, op0=ALU.add)
+            nc.vector.scalar_tensor_tensor(
+                out=rest_low[:], in0=t_col, scalar=W_LOW, in1=r_col, op0=ALU.mult, op1=ALU.add
+            )
+            nc.vector.scalar_tensor_tensor(
+                out=rest_high[:], in0=t_col, scalar=W_HIGH, in1=r_col, op0=ALU.mult, op1=ALU.add
+            )
+            nc.vector.tensor_tensor(out=shift[:], in0=t_col, in1=b_col, op=ALU.mult)
+            nc.vector.tensor_tensor(out=low[:], in0=rest_low[:], in1=rest_high[:], op=ALU.min)
+            nc.vector.tensor_tensor(out=high[:], in0=rest_low[:], in1=rest_high[:], op=ALU.max)
+            nc.vector.tensor_tensor(out=shift[:], in0=shift[:], in1=r_col, op=ALU.add)
+
+        def columns_to_rows():
+            for row, col in ((bias_row, bias_up[:]), (travel_row, t_col), (rest_row, rest_low[:])):
+                bank = psum.tile([P, 512], F32, name="row_bank", tag="acc", bufs=ACC)
+                for b in range(BLOCKS):
+                    nc.tensor.transpose(
+                        bank[:, P * b : P * (b + 1)], col[:, b : b + 1].to_broadcast([P, P]), ident[:]
+                    )
+                if row is rest_row:
+                    nc.vector.tensor_copy(out=row[:], in_=bank[:])
+                else:
+                    nc.scalar.copy(out=row[:], in_=bank[:])
+
+        def solver_group(h):
+            nc.vector.tensor_copy(out=solver_grp[h][:], in_=solver_raw[h][:].rearrange("p j n -> p n j"))
+
+        def solver_quantize(h):
+            nc.vector.quantize_mx(
+                out=solver_codes[h][:].bitcast(FP8X4),
+                scales=solver_sc[h][:],
+                in_=solver_grp[h][:].rearrange("p n j -> p (n j)"),
+            )
+
+        grouped, split = {}, {}
+
+        def head_turn(j):
+            new = work.tile([P, PASSES, P, 4], BF16, name="grouped_h", tag="grouped", bufs=4, align_bytes=64)
+            grouped["h", j] = new
+            pairs = head_raw[j][:].bitcast(F32)
+            gw = new[:].rearrange("p c r t -> p (c r t)").bitcast(F32).rearrange(
+                "p (c r u) -> p c r u", c=PASSES, u=2
+            )
+            for b in range(2):
+                bank = psum.tile([P, 2, 2, P], F32, name="x_bank", tag="xt", bufs=XT)
+                for cc in range(2):
+                    for u in range(2):
+                        base = 256 * (2 * b + cc)
+                        nc.tensor.transpose(bank[:, cc, u, :], pairs[:, base + u : base + 256 : 2], ident[:])
+                nc.scalar.copy(out=gw[:, 2 * b : 2 * b + 2, :, :], in_=bank[:].rearrange("p c u r -> p c r u"))
+
+        def head_quantize(j):
+            for c in range(PASSES):
+                nc.vector.quantize_mx(
+                    out=codes[0][:, c, P * j : P * (j + 1)].bitcast(FP8X4),
+                    scales=scales[0][:, c, P * j : P * (j + 1)],
+                    in_=grouped["h", j][:, c, :, :].rearrange("p r t -> p (r t)"),
+                )
+
+        def unit_split(n):
+            new = work.tile([P, TILES, 2, P], F32, name="split", bufs=2, align_bytes=64)
+            split[n] = new
+            nc.vector.tensor_copy(
+                out=new[:],
+                in_=raw[n // 4 + 1, n % 4][:].bitcast(F32).rearrange("p j (m u) -> p j u m", u=2),
+            )
+
+        def unit_turn(n):
+            new = work.tile([P, TILES, P, 4], BF16, name="grouped_u", tag="grouped", bufs=4, align_bytes=64)
+            grouped[n] = new
+            gw = new[:].rearrange("p j r t -> p (j r t)").bitcast(F32).rearrange(
+                "p (j r u) -> p j r u", j=TILES, u=2
+            )
+            for b in range(2):
+                bank = psum.tile([P, 2, 2, P], F32, name="x_bank", tag="xt", bufs=XT)
+                for jj in range(2):
+                    for u in range(2):
+                        nc.tensor.transpose(bank[:, jj, u, :], split[n][:, 2 * b + jj, u, :], ident[:])
+                nc.scalar.copy(out=gw[:, 2 * b : 2 * b + 2, :, :], in_=bank[:].rearrange("p j u r -> p j r u"))
+
+        def unit_quantize(n):
+            g, c = n // 4 + 1, n % 4
+            nc.vector.quantize_mx(
+                out=codes[g][:, c, :].bitcast(FP8X4),
+                scales=scales[g][:, c, :],
+                in_=grouped[n][:].rearrange("p j r t -> p (j r t)"),
+            )
+
+        def weight(c, h, c0, c1):
+            if c < SKIN_PASSES:
+                base = N * c + HALF * h
+                return words[h][:, c, 2 * c0 : 2 * c1].bitcast(FP4X4), skin_sc[:, base + c0 : base + c1]
+            return solver_codes[h][:, c0:c1].bitcast(FP8X4), solver_sc[h][:, c0:c1]
+
+        def frames(g, c, t0, t1):
+            return codes[g][:, c, t0:t1].bitcast(FP8X4), scales[g][:, c, t0:t1]
+
+        def product(acc, lhs, rhs, c):
+            nc.tensor.matmul_mx(
+                out=acc[:], lhsT=lhs[0], lhsT_scale=lhs[1], rhs=rhs[0], rhs_scale=rhs[1],
+                start=(c == 0), stop=(c == PASSES - 1),
+            )
+
+        acc_t, acc_c, xs, ys, zs, as_, vs, o_c = {}, {}, {}, {}, {}, {}, {}, {}
+
+        def t_mm(i):
+            new = psum.tile([P, 512], F32, name="acc_t", tag="acc", bufs=ACC)
+            acc_t[i] = new
+            g, j = i // 4, i % 4
+            for c in range(PASSES):
+                product(new, frames(g, c, P * j, P * (j + 1)), weight(c, 0, 0, HALF), c)
+
+        def t_bias(i):
+            new = work.tile([P, HALF], F32, name="x", bufs=4, align_bytes=64)
+            xs[i] = new
+            nc.vector.tensor_tensor(out=new[:], in0=acc_t[i][:], in1=bias_row[:], op=ALU.add)
+
+        def t_relu(i):
+            new = work.tile([P, HALF], F32, name="y", bufs=4, align_bytes=64)
+            ys[i] = new
+            nc.scalar.activation(out=new[:], in_=xs[i][:], func=ACT.Relu)
+
+        def t_scale(i):
+            new = work.tile([P, HALF], F32, name="z", bufs=4, align_bytes=64)
+            zs[i] = new
+            nc.vector.scalar_tensor_tensor(
+                out=new[:], in0=ys[i][:], scalar=W_HIGH - W_LOW, in1=travel_row[:], op0=ALU.min, op1=ALU.mult
+            )
+
+        def t_rest(i):
+            o = work.tile([P, HALF], F32, name="o", bufs=6, align_bytes=64)
+            nc.vector.tensor_tensor(out=o[:], in0=zs[i][:], in1=rest_row[:], op=ALU.add)
+            nc.sync.dma_start(out=group_rows(out, i // 4)[:, i % 4, 0:HALF], in_=o[:])
+
+        def c_mm(i):
+            new = psum.tile([P, 512], F32, name="acc_c", tag="acc", bufs=ACC)
+            acc_c[i] = new
+            g, b = i // 4, i % 4
+            for c in range(PASSES):
+                product(new, weight(c, 1, P * b, P * (b + 1)), frames(g, c, 0, GROUP), c)
+
+        def c_affine(i):
+            new = work.tile([P, GROUP], F32, name="a", bufs=4, align_bytes=64)
+            as_[i] = new
+            k = BLOCKS + i % 4
+            nc.scalar.activation(
+                out=new[:], in_=acc_c[i][:], func=ACT.Identity, bias=shift[:, k : k + 1], scale=cols[:, 8 + k : 9 + k]
+            )
+
+        def c_clamp(i):
+            new = work.tile([P, GROUP], F32, name="v", bufs=4, align_bytes=64)
+            vs[i] = new
+            k = BLOCKS + i % 4
+            nc.vector.tensor_scalar(
+                out=new[:], in0=as_[i][:], scalar1=low[:, k : k + 1], scalar2=high[:, k : k + 1],
+                op0=ALU.max, op1=ALU.min,
+            )
+
+        def c_back(i):
+            g, b = i // 4, i % 4
+            bank = psum.tile([P, TILES, P], F32, name="back", tag="back", bufs=BACK)
+            acc_c[i] = bank
+            for j in range(TILES):
+                nc.tensor.transpose(bank[:, j, :], vs[i][:, P * j : P * (j + 1)], ident[:])
+
+        def c_out(i):
+            g, b = i // 4, i % 4
+            if b == 0:
+                new = work.tile([P, TILES, HALF], F32, name="o_c", bufs=2, align_bytes=64)
+                o_c[g] = new
+            nc.scalar.copy(out=o_c[g][:, :, P * b : P * (b + 1)], in_=acc_c[i][:])
+            if b % 2 == 1:
+                nc.sync.dma_start(
+                    out=group_rows(out, g)[:, :, HALF + P * (b - 1) : HALF + P * (b + 1)],
+                    in_=o_c[g][:, :, P * (b - 1) : P * (b + 1)],
+                )
+
+        with tc.manual_schedule():
+            vectors_to_columns()
+            columns_to_rows()
+            head_turn(0)
+            solver_group(0)
+            head_quantize(0)
+            solver_quantize(0)
+            head_turn(1)
+            t_mm(0)
+            solver_group(1)
+            head_quantize(1)
+            t_bias(0)
+            solver_quantize(1)
+            head_turn(2)
+            t_relu(0)
+            head_quantize(2)
+            t_mm(1)
+            t_scale(0)
+            t_bias(1)
+            t_rest(0)
+            head_turn(3)
+            t_relu(1)
+            unit_split(0)
+            head_quantize(3)
+            t_mm(2)
+            t_scale(1)
+            t_bias(2)
+            t_rest(1)
+            unit_turn(0)
+            t_relu(2)
+            unit_quantize(0)
+            t_mm(3)
+            t_scale(2)
+            unit_split(1)
+            t_rest(2)
+            t_bias(3)
+            c_mm(0)
+            c_mm(1)
+            c_affine(0)
+            unit_split(2)
+            c_clamp(0)
+            c_affine(1)
+            unit_turn(1)
+            t_relu(3)
+            unit_quantize(1)
+            c_mm(2)
+            c_affine(2)
+            t_scale(3)
+            c_clamp(1)
+            unit_turn(2)
+            c_back(0)
+            c_out(0)
+            t_rest(3)
+            c_clamp(2)
+            unit_split(3)
+            unit_quantize(2)
+            c_mm(3)
+            unit_turn(3)
+            c_back(1)
+            c_out(1)
+            unit_split(4)
+            unit_quantize(3)
+            for i in range(4, 16):
+                c_affine(i - 1)
+                if i > 4:
+                    t_bias(i - 1)
+                if i > 5:
+                    t_rest(i - 2)
+                if i < 12:
+                    unit_turn(i)
+                if i + 1 < 12:
+                    unit_split(i + 1)
+                c_clamp(i - 1)
+                c_back(i - 2)
+                if i > 4:
+                    t_relu(i - 1)
+                c_out(i - 2)
+                if i < 12:
+                    unit_quantize(i)
+                if i > 4:
+                    t_scale(i - 1)
+                t_mm(i)
+                c_mm(i)
+            t_bias(15)
+            c_affine(15)
+            t_rest(14)
+            c_clamp(15)
+            c_back(14)
+            t_relu(15)
+            c_out(14)
+            t_scale(15)
+            c_back(15)
+            c_out(15)
+            t_rest(15)
+
+
+XT, ACC, BACK = 2, 4, 2

@@ -46,8 +46,6 @@ def tile_face_retarget_rig_s1_kernel(
         make_identity(nc, ident[:])
         nc.scalar.activation(out=warm[:], in_=warm[:], func=ACT.Relu)
 
-        for v, vec in enumerate((actor_bias, travel, rest)):
-            nc.sync.dma_start(out=vec_rows[8 * v : 8 * v + 8, :], in_=vec.rearrange("(c p) -> c p", p=P))
 
         words = [keep.tile([P, SKIN_PASSES, 2 * HALF], U8, name=f"words{h}", align_bytes=64) for h in range(2)]
         solver_raw = [keep.tile([P, 4, HALF], BF16, name=f"solver_raw{h}", align_bytes=64) for h in range(2)]
@@ -80,7 +78,7 @@ def tile_face_retarget_rig_s1_kernel(
             dst = skin_sc[:].bitcast(I32).rearrange("p (g n) -> p g n", g=SKIN_PASSES)
             src = skin_scales.bitcast(I32)
             for q in range(4):
-                nc.sync.dma_start(
+                nc.scalar.dma_start(
                     out=dst[32 * q : 32 * q + 4, :, :],
                     in_=src[:, 4 * q : 4 * q + 4, :].rearrange("g r n -> r g n"),
                 )
@@ -92,9 +90,11 @@ def tile_face_retarget_rig_s1_kernel(
             )
 
         load_head(0)
-        load_scales()
-        load_solver(0)
+        for v, vec in enumerate((actor_bias, travel, rest)):
+            nc.scalar.dma_start(out=vec_rows[8 * v : 8 * v + 8, :], in_=vec.rearrange("(c p) -> c p", p=P))
         load_words(0)
+        load_solver(0)
+        load_scales()
         load_head(1)
         load_solver(1)
         load_head(2)
@@ -135,20 +135,21 @@ def tile_face_retarget_rig_s1_kernel(
             nc.vector.tensor_tensor(out=high[:], in0=rest_low[:], in1=rest_high[:], op=ALU.max)
             nc.vector.tensor_tensor(out=shift[:], in0=shift[:], in1=r_col, op=ALU.add)
 
-        def columns_to_rows():
-            for row, col in ((bias_row, bias_up[:]), (travel_row, t_col), (rest_row, rest_low[:])):
-                bank = psum.tile([P, 512], F32, name="row_bank", tag="acc", bufs=ACC)
-                for b in range(BLOCKS):
-                    nc.tensor.transpose(
-                        bank[:, P * b : P * (b + 1)], col[:, b : b + 1].to_broadcast([P, P]), ident[:]
-                    )
-                if row is rest_row:
-                    nc.vector.tensor_copy(out=row[:], in_=bank[:])
-                else:
-                    nc.scalar.copy(out=row[:], in_=bank[:])
+        def column_to_row(row, col, tag="back", bufs=2):
+            bank = psum.tile([P, 512], F32, name="row_bank", tag=tag, bufs=bufs)
+            for b in range(BLOCKS):
+                nc.tensor.transpose(bank[:, P * b : P * (b + 1)], col[:, b : b + 1].to_broadcast([P, P]), ident[:])
+            return bank
+
+        def row_copy(row, bank):
+            nc.vector.tensor_copy(out=row[:], in_=bank[:])
 
         def solver_group(h):
-            nc.vector.tensor_copy(out=solver_grp[h][:], in_=solver_raw[h][:].rearrange("p j n -> p n j"))
+            src = solver_raw[h][:].rearrange("p j n -> p n j")
+            if h == 0:
+                nc.scalar.copy(out=solver_grp[h][:], in_=src)
+            else:
+                nc.vector.tensor_copy(out=solver_grp[h][:], in_=src)
 
         def solver_quantize(h):
             nc.vector.quantize_mx(
@@ -191,6 +192,7 @@ def tile_face_retarget_rig_s1_kernel(
             )
 
         def unit_turn(n):
+            words_of = raw[n // 4 + 1, n % 4][:].bitcast(F32)
             new = work.tile([P, TILES, P, 4], BF16, name="grouped_u", tag="grouped", bufs=4, align_bytes=64)
             grouped[n] = new
             gw = new[:].rearrange("p j r t -> p (j r t)").bitcast(F32).rearrange(
@@ -200,7 +202,8 @@ def tile_face_retarget_rig_s1_kernel(
                 bank = psum.tile([P, 2, 2, P], F32, name="x_bank", tag="xt", bufs=XT)
                 for jj in range(2):
                     for u in range(2):
-                        nc.tensor.transpose(bank[:, jj, u, :], split[n][:, 2 * b + jj, u, :], ident[:])
+                        src = split[n][:, 2 * b + jj, u, :] if n in split else words_of[:, 2 * b + jj, u : 256 : 2]
+                        nc.tensor.transpose(bank[:, jj, u, :], src, ident[:])
                 nc.scalar.copy(out=gw[:, 2 * b : 2 * b + 2, :, :], in_=bank[:].rearrange("p j u r -> p j r u"))
 
         def unit_quantize(n):
@@ -228,12 +231,13 @@ def tile_face_retarget_rig_s1_kernel(
 
         acc_t, acc_c, xs, ys, zs, as_, vs, o_c = {}, {}, {}, {}, {}, {}, {}, {}
 
-        def t_mm(i):
-            new = psum.tile([P, 512], F32, name="acc_t", tag="acc", bufs=ACC)
-            acc_t[i] = new
+        def t_mm(i, passes=range(PASSES)):
+            if passes[0] == 0:
+                new = psum.tile([P, 512], F32, name="acc_t", tag="acc", bufs=ACC)
+                acc_t[i] = new
             g, j = i // 4, i % 4
-            for c in range(PASSES):
-                product(new, frames(g, c, P * j, P * (j + 1)), weight(c, 0, 0, HALF), c)
+            for c in passes:
+                product(acc_t[i], frames(g, c, P * j, P * (j + 1)), weight(c, 0, 0, HALF), c)
 
         def t_bias(i):
             new = work.tile([P, HALF], F32, name="x", bufs=4, align_bytes=64)
@@ -290,78 +294,135 @@ def tile_face_retarget_rig_s1_kernel(
 
         def c_out(i):
             g, b = i // 4, i % 4
-            if b == 0:
-                new = work.tile([P, TILES, HALF], F32, name="o_c", bufs=2, align_bytes=64)
-                o_c[g] = new
-            nc.scalar.copy(out=o_c[g][:, :, P * b : P * (b + 1)], in_=acc_c[i][:])
+            if b % 2 == 0:
+                new = work.tile([P, TILES, 2, P], F32, name="o_c", bufs=4, align_bytes=64)
+                o_c[i // 2] = new
+            pair = o_c[i // 2]
+            nc.scalar.copy(out=pair[:, :, b % 2, :], in_=acc_c[i][:])
             if b % 2 == 1:
                 nc.sync.dma_start(
                     out=group_rows(out, g)[:, :, HALF + P * (b - 1) : HALF + P * (b + 1)],
-                    in_=o_c[g][:, :, P * (b - 1) : P * (b + 1)],
+                    in_=pair[:].rearrange("p j b n -> p j (b n)"),
                 )
 
+        def last_c():
+            i = 15
+            g, b, k = 3, 3, BLOCKS + 3
+            accs, ys_, banks = [], [], []
+            for e in range(2):
+                acc = psum.tile([P, 2, P], F32, name=f"acc_l{e}", tag="xt", bufs=XT)
+                accs.append(acc)
+                for jj in range(2):
+                    t0 = P * (2 * e + jj)
+                    for c in range(PASSES):
+                        lhs, rhs = weight(c, 1, P * b, P * (b + 1)), frames(g, c, t0, t0 + P)
+                        nc.tensor.matmul_mx(
+                            out=acc[:, jj, :], lhsT=lhs[0], lhsT_scale=lhs[1], rhs=rhs[0], rhs_scale=rhs[1],
+                            start=(c == 0), stop=(c == PASSES - 1),
+                        )
+            return accs
+
+        def last_affine(accs, e):
+            k = BLOCKS + 3
+            a = work.tile([P, 2 * P], F32, name=f"a_l{e}", tag="a", bufs=4, align_bytes=64)
+            nc.scalar.activation(
+                out=a[:], in_=accs[e][:].rearrange("p j r -> p (j r)"), func=ACT.Identity,
+                bias=shift[:, k : k + 1], scale=cols[:, 8 + k : 9 + k],
+            )
+            return a
+
+        def last_clamp(a, e):
+            k = BLOCKS + 3
+            v = work.tile([P, 2 * P], F32, name=f"v_l{e}", tag="v", bufs=4, align_bytes=64)
+            nc.vector.tensor_scalar(
+                out=v[:], in0=a[:], scalar1=low[:, k : k + 1], scalar2=high[:, k : k + 1], op0=ALU.max, op1=ALU.min
+            )
+            return v
+
+        def last_back(v, e):
+            bank = psum.tile([P, 2, P], F32, name=f"back_l{e}", tag="back", bufs=BACK)
+            for jj in range(2):
+                nc.tensor.transpose(bank[:, jj, :], v[:, P * jj : P * (jj + 1)], ident[:])
+            return bank
+
+        def last_out(bank, e):
+            o = work.tile([P, 2, P], F32, name=f"o_l{e}", tag="o", bufs=6, align_bytes=64)
+            eng = nc.scalar.copy if e else nc.vector.tensor_copy
+            eng(out=o[:], in_=bank[:])
+            nc.sync.dma_start(out=group_rows(out, 3)[:, 2 * e : 2 * e + 2, HALF + 3 * P : N], in_=o[:])
+
+        def c_out_single(i):
+            o = work.tile([P, TILES, P], F32, name="o_s", tag="o", bufs=6, align_bytes=64)
+            nc.scalar.copy(out=o[:], in_=acc_c[i][:])
+            nc.sync.dma_start(out=group_rows(out, 3)[:, :, HALF + 2 * P : HALF + 3 * P], in_=o[:])
+
         with tc.manual_schedule():
-            vectors_to_columns()
-            columns_to_rows()
             head_turn(0)
-            solver_group(0)
+            vectors_to_columns()
             head_quantize(0)
-            solver_quantize(0)
+            solver_group(0)
+            bb = column_to_row(bias_row, bias_up[:])
+            tb = column_to_row(travel_row, t_col)
+            rb = column_to_row(rest_row, rest_low[:], "acc", 4)
+            row_copy(bias_row, bb)
+            row_copy(travel_row, tb)
+            row_copy(rest_row, rb)
+            t_mm(0, range(3))
             head_turn(1)
-            t_mm(0)
+            solver_quantize(0)
+            t_mm(0, range(3, 4))
             solver_group(1)
             head_quantize(1)
             t_bias(0)
-            solver_quantize(1)
             head_turn(2)
             t_relu(0)
-            head_quantize(2)
             t_mm(1)
-            t_scale(0)
+            solver_quantize(1)
+            head_quantize(2)
             t_bias(1)
-            t_rest(0)
+            t_scale(0)
             head_turn(3)
             t_relu(1)
-            unit_split(0)
-            head_quantize(3)
             t_mm(2)
-            t_scale(1)
+            t_rest(0)
+            head_quantize(3)
             t_bias(2)
-            t_rest(1)
-            unit_turn(0)
+            t_scale(1)
             t_relu(2)
-            unit_quantize(0)
-            t_mm(3)
-            t_scale(2)
             unit_split(1)
-            t_rest(2)
+            unit_turn(0)
+            t_mm(3)
             t_bias(3)
-            c_mm(0)
-            c_mm(1)
-            c_affine(0)
-            unit_split(2)
-            c_clamp(0)
-            c_affine(1)
-            unit_turn(1)
             t_relu(3)
+            unit_quantize(0)
+            unit_split(2)
+            t_rest(1)
+            t_scale(2)
+            c_mm(0)
+            unit_turn(1)
+            c_affine(0)
+            c_mm(1)
+            c_clamp(0)
             unit_quantize(1)
-            c_mm(2)
-            c_affine(2)
-            t_scale(3)
-            c_clamp(1)
+            c_affine(1)
+            unit_split(3)
+            t_rest(2)
             unit_turn(2)
             c_back(0)
             c_out(0)
-            t_rest(3)
-            c_clamp(2)
-            unit_split(3)
+            c_mm(2)
+            c_clamp(1)
             unit_quantize(2)
-            c_mm(3)
+            t_scale(3)
+            c_affine(2)
             unit_turn(3)
             c_back(1)
             c_out(1)
+            c_mm(3)
+            c_clamp(2)
             unit_split(4)
             unit_quantize(3)
+            t_rest(3)
             for i in range(4, 16):
                 c_affine(i - 1)
                 if i > 4:
@@ -382,18 +443,24 @@ def tile_face_retarget_rig_s1_kernel(
                 if i > 4:
                     t_scale(i - 1)
                 t_mm(i)
-                c_mm(i)
+                if i < 15:
+                    c_mm(i)
+            accs = last_c()
             t_bias(15)
-            c_affine(15)
-            t_rest(14)
-            c_clamp(15)
-            c_back(14)
             t_relu(15)
-            c_out(14)
+            t_rest(14)
+            c_back(14)
+            a0 = last_affine(accs, 0)
             t_scale(15)
-            c_back(15)
-            c_out(15)
+            a1 = last_affine(accs, 1)
+            v0 = last_clamp(a0, 0)
+            c_out_single(14)
+            v1 = last_clamp(a1, 1)
             t_rest(15)
+            b0 = last_back(v0, 0)
+            b1 = last_back(v1, 1)
+            last_out(b0, 0)
+            last_out(b1, 1)
 
 
 XT, ACC, BACK = 2, 4, 2

@@ -21,10 +21,13 @@ KP = 512
 SKIN_PASSES = D // KP
 PASSES = SKIN_PASSES + 1
 GROUP = 512
+GROUPS = T // GROUP
 TILES = GROUP // P
-HALF = 512
+HALF = N // 2
 BLOCKS = HALF // P
+UNITS = GROUPS * TILES
 W_LOW, W_HIGH = -0.5, 1.0
+TURN_BANKS, ACC_BANKS = 2, 4
 
 
 def tile_face_retarget_rig_s1_kernel(
@@ -35,432 +38,465 @@ def tile_face_retarget_rig_s1_kernel(
         keep = ctx.enter_context(tc.tile_pool(name="keep", bufs=1))
         work = ctx.enter_context(tc.tile_pool(name="work", bufs=3))
         psum = ctx.enter_context(tc.psum_pool(name="psum", bufs=1))
+        ctx.enter_context(tc.manual_schedule())
 
-        skin_sc = keep.tile([P, SKIN_PASSES * N], U8, align_bytes=64)
-        vec_rows = keep.tile([P, P], BF16, align_bytes=64)
-        ident = keep.tile([P, P], F32, align_bytes=64)
-        warm = keep.tile([P, 1], F32)
-        nc.vector.memset(vec_rows[:], 0.0)
-        nc.vector.memset(skin_sc[:].bitcast(I32), 0)
-        nc.vector.memset(warm[:], 0.0)
-        make_identity(nc, ident[:])
-        nc.scalar.activation(out=warm[:], in_=warm[:], func=ACT.Relu)
+        def kept(name, shape, dtype):
+            return keep.tile(shape, dtype, name=name, align_bytes=256)
 
+        def turn_bank(name, shape):
+            return psum.tile(shape, F32, name=name, tag="turn", bufs=TURN_BANKS)
 
-        words = [keep.tile([P, SKIN_PASSES, 2 * HALF], U8, name=f"words{h}", align_bytes=64) for h in range(2)]
-        solver_raw = [keep.tile([P, 4, HALF], BF16, name=f"solver_raw{h}", align_bytes=64) for h in range(2)]
-        solver_grp = [keep.tile([P, HALF, 4], BF16, name=f"solver_grp{h}", align_bytes=64) for h in range(2)]
-        solver_codes = [keep.tile([P, HALF], U32, name=f"solver_codes{h}", align_bytes=64) for h in range(2)]
-        solver_sc = [keep.tile([P, HALF], U8, name=f"solver_sc{h}", align_bytes=64) for h in range(2)]
-        codes = [keep.tile([P, PASSES, GROUP], U32, name=f"codes{g}", align_bytes=64) for g in range(4)]
-        scales = [keep.tile([P, PASSES, GROUP], U8, name=f"scales{g}", align_bytes=64) for g in range(4)]
-        head_raw = [keep.tile([P, D + C], BF16, name=f"head_raw{j}", align_bytes=64) for j in range(TILES)]
-        raw = {
-            (g, c): keep.tile([P, TILES, KP], BF16, name=f"raw{g}_{c}", align_bytes=64)
-            for g in range(1, 4)
-            for c in range(PASSES)
-        }
+        def back_bank(name, shape):
+            return psum.tile(shape, F32, name=name, tag="back", bufs=2)
+
+        def acc_bank(name, shape=(P, 512)):
+            return psum.tile(list(shape), F32, name=name, tag="acc", bufs=ACC_BANKS)
 
         def group_rows(x, g):
             return x[GROUP * g : GROUP * (g + 1), :].rearrange("(p j) k -> p j k", j=TILES)
 
-        def load_head(j):
-            nc.sync.dma_start(out=head_raw[j][:, 0:D], in_=group_rows(skin, 0)[:, j, :])
-            nc.sync.dma_start(out=head_raw[j][:, D : D + C], in_=group_rows(lips, 0)[:, j, :])
+        ident = kept("ident", [P, P], F32)
+        warm_in = kept("warm_in", [P, 4 * P], BF16)
+        warm_codes = kept("warm_codes", [P, P], U32)
+        warm_scales = kept("warm_scales", [P, P], U8)
+        vec_rows = kept("vec_rows", [P, P], BF16)
+        word_scales = kept("word_scales", [P, SKIN_PASSES * N], U8)
+        words = [kept(f"words{h}", [P, SKIN_PASSES, 2 * HALF], U8) for h in range(2)]
+        solver_raw = [kept(f"solver_raw{h}", [P, 4, HALF], BF16) for h in range(2)]
+        solver_grouped = [kept(f"solver_grouped{h}", [P, HALF, 4], BF16) for h in range(2)]
+        solver_codes = [kept(f"solver_codes{h}", [P, HALF], U32) for h in range(2)]
+        solver_scales = [kept(f"solver_scales{h}", [P, HALF], U8) for h in range(2)]
+        codes = [kept(f"codes{g}", [P, PASSES, GROUP], U32) for g in range(GROUPS)]
+        scales = [kept(f"scales{g}", [P, PASSES, GROUP], U8) for g in range(GROUPS)]
+        tile_raw = [kept(f"tile_raw{j}", [P, D + C], BF16) for j in range(TILES)]
+        pass_raw = [kept(f"pass_raw{n}", [P, TILES, KP], BF16) for n in range((GROUPS - 1) * PASSES)]
+
+        nc.vector.memset(warm_in[:], 1.0)
+        for tile in (word_scales, vec_rows):
+            nc.vector.memset(tile[:].bitcast(I32), 0)
+        make_identity(nc, ident[:])
+
+        def load_tile(j):
+            nc.sync.dma_start(out=tile_raw[j][:, 0:D], in_=group_rows(skin, 0)[:, j, :])
+            nc.sync.dma_start(out=tile_raw[j][:, D : D + C], in_=group_rows(lips, 0)[:, j, :])
 
         def load_words(h):
-            nc.sync.dma_start(
-                out=words[h][:],
-                in_=skin_words.rearrange("g p n -> p g n")[:, :, 2 * HALF * h : 2 * HALF * (h + 1)],
-            )
+            by_row = skin_words.rearrange("g p n -> p g n")
+            nc.sync.dma_start(out=words[h][:], in_=by_row[:, :, 2 * HALF * h : 2 * HALF * (h + 1)])
 
-        def load_scales():
-            dst = skin_sc[:].bitcast(I32).rearrange("p (g n) -> p g n", g=SKIN_PASSES)
-            src = skin_scales.bitcast(I32)
+        def load_word_scales():
+            dst = word_scales[:].bitcast(I32).rearrange("p (g n) -> p g n", g=SKIN_PASSES)
+            src = skin_scales.bitcast(I32).rearrange("g q n -> q g n")
             for q in range(4):
-                nc.scalar.dma_start(
-                    out=dst[32 * q : 32 * q + 4, :, :],
-                    in_=src[:, 4 * q : 4 * q + 4, :].rearrange("g r n -> r g n"),
-                )
+                nc.scalar.dma_start(out=dst[32 * q : 32 * q + 4, :, :], in_=src[4 * q : 4 * q + 4, :, :])
 
         def load_solver(h):
-            nc.sync.dma_start(
-                out=solver_raw[h][:],
-                in_=lip_solver.rearrange("(p j) n -> p j n", j=4)[:, :, HALF * h : HALF * (h + 1)],
-            )
+            by_word = lip_solver.rearrange("(p t) n -> p t n", t=4)
+            nc.sync.dma_start(out=solver_raw[h][:], in_=by_word[:, :, HALF * h : HALF * (h + 1)])
 
-        load_head(0)
-        for v, vec in enumerate((actor_bias, travel, rest)):
-            nc.scalar.dma_start(out=vec_rows[8 * v : 8 * v + 8, :], in_=vec.rearrange("(c p) -> c p", p=P))
+        def load_vectors():
+            for v, vec in enumerate((actor_bias, travel, rest)):
+                nc.gpsimd.dma_start(out=vec_rows[8 * v : 8 * v + 8, :], in_=vec.rearrange("(b n) -> b n", n=P))
+
+        def load_pass(n):
+            g, c = n // PASSES + 1, n % PASSES
+            source = group_rows(skin, g)[:, :, KP * c : KP * (c + 1)] if c < SKIN_PASSES else group_rows(lips, g)
+            nc.sync.dma_start(out=pass_raw[n][:], in_=source)
+
+        load_word_scales()
+        load_tile(0)
+        load_vectors()
         load_words(0)
         load_solver(0)
-        load_scales()
-        load_head(1)
+        load_tile(1)
         load_solver(1)
-        load_head(2)
-        load_head(3)
+        load_tile(2)
+        load_tile(3)
         load_words(1)
-        for g in range(1, 4):
-            for c in range(PASSES):
-                src = group_rows(skin, g)[:, :, KP * c : KP * (c + 1)] if c < SKIN_PASSES else group_rows(lips, g)
-                nc.sync.dma_start(out=raw[g, c][:], in_=src)
+        for n in range((GROUPS - 1) * PASSES):
+            load_pass(n)
 
-        vec_f32 = keep.tile([P, P], F32, align_bytes=64)
-        cols = keep.tile([P, 24], F32, align_bytes=64)
-        bias_up = keep.tile([P, 8], F32)
-        rest_low = keep.tile([P, 8], F32)
-        rest_high = keep.tile([P, 8], F32)
-        shift = keep.tile([P, 8], F32)
-        low = keep.tile([P, 8], F32)
-        high = keep.tile([P, 8], F32)
-        bias_row = keep.tile([P, HALF], F32, align_bytes=64)
-        travel_row = keep.tile([P, HALF], F32, align_bytes=64)
-        rest_row = keep.tile([P, HALF], F32, align_bytes=64)
-        b_col, t_col, r_col = cols[:, 0:8], cols[:, 8:16], cols[:, 16:24]
+        cols = kept("cols", [P, 24], F32)
+        bias_col, travel_col, rest_col = cols[:, 0:8], cols[:, 8:16], cols[:, 16:24]
+        raised_bias_col = kept("raised_bias_col", [P, 8], F32)
+        floor_col = kept("floor_col", [P, 8], F32)
+        ceil_col = kept("ceil_col", [P, 8], F32)
+        shift_col = kept("shift_col", [P, 8], F32)
+        low_col = kept("low_col", [P, 8], F32)
+        high_col = kept("high_col", [P, 8], F32)
+        raised_bias_row = kept("raised_bias_row", [P, HALF], F32)
+        travel_row = kept("travel_row", [P, HALF], F32)
+        floor_row = kept("floor_row", [P, HALF], F32)
 
-        def vectors_to_columns():
+        def warm_quant():
+            nc.vector.quantize_mx(out=warm_codes[:].bitcast(FP8X4), scales=warm_scales[:], in_=warm_in[:])
+
+        def warm_up(count):
+            bank = acc_bank("warm_bank")
+            for i in range(count):
+                nc.tensor.matmul_mx(
+                    out=bank[:, 0:P],
+                    lhsT=warm_codes[:].bitcast(FP8X4),
+                    lhsT_scale=warm_scales[:],
+                    rhs=warm_codes[:].bitcast(FP8X4),
+                    rhs_scale=warm_scales[:],
+                    start=True,
+                    stop=True,
+                )
+
+        vec_f32 = kept("vec_f32", [P, P], F32)
+
+        def widen_vectors():
             nc.vector.tensor_copy(out=vec_f32[:], in_=vec_rows[:])
-            bank = psum.tile([P, 512], F32, name="vec_bank", tag="back", bufs=BACK)
-            nc.tensor.transpose(bank[:, 0:P], vec_f32[:], ident[:])
+
+        def turn_vectors():
+            bank = back_bank("vec_bank", [P, P])
+            nc.tensor.transpose(bank[:], vec_f32[:], ident[:])
             nc.vector.tensor_copy(out=cols[:], in_=bank[:, 0:24])
-            nc.vector.tensor_scalar(out=bias_up[:], in0=b_col, scalar1=-W_LOW, scalar2=None, op0=ALU.add)
-            nc.vector.scalar_tensor_tensor(
-                out=rest_low[:], in0=t_col, scalar=W_LOW, in1=r_col, op0=ALU.mult, op1=ALU.add
+
+        def derive_columns():
+            nc.vector.tensor_scalar(
+                out=raised_bias_col[:], in0=bias_col, scalar1=-W_LOW, scalar2=None, op0=ALU.add
             )
-            nc.vector.scalar_tensor_tensor(
-                out=rest_high[:], in0=t_col, scalar=W_HIGH, in1=r_col, op0=ALU.mult, op1=ALU.add
-            )
-            nc.vector.tensor_tensor(out=shift[:], in0=t_col, in1=b_col, op=ALU.mult)
-            nc.vector.tensor_tensor(out=low[:], in0=rest_low[:], in1=rest_high[:], op=ALU.min)
-            nc.vector.tensor_tensor(out=high[:], in0=rest_low[:], in1=rest_high[:], op=ALU.max)
-            nc.vector.tensor_tensor(out=shift[:], in0=shift[:], in1=r_col, op=ALU.add)
+            for col, weight in ((floor_col, W_LOW), (ceil_col, W_HIGH)):
+                nc.vector.scalar_tensor_tensor(
+                    out=col[:], in0=travel_col, scalar=weight, in1=rest_col, op0=ALU.mult, op1=ALU.add
+                )
+            moved = work.tile([P, 8], F32, name="moved", bufs=1)
+            nc.vector.tensor_tensor(out=moved[:], in0=travel_col, in1=bias_col, op=ALU.mult)
+            nc.vector.tensor_tensor(out=low_col[:], in0=floor_col[:], in1=ceil_col[:], op=ALU.min)
+            nc.vector.tensor_tensor(out=high_col[:], in0=floor_col[:], in1=ceil_col[:], op=ALU.max)
+            nc.vector.tensor_tensor(out=shift_col[:], in0=moved[:], in1=rest_col, op=ALU.add)
 
-        def column_to_row(row, col, tag="back", bufs=2):
-            bank = psum.tile([P, 512], F32, name="row_bank", tag=tag, bufs=bufs)
-            for b in range(BLOCKS):
-                nc.tensor.transpose(bank[:, P * b : P * (b + 1)], col[:, b : b + 1].to_broadcast([P, P]), ident[:])
-            return bank
+        row_banks = {}
 
-        def row_copy(row, bank):
-            nc.vector.tensor_copy(out=row[:], in_=bank[:])
+        def turn_row(v, new_bank):
+            col = (raised_bias_col[:], travel_col, floor_col[:])[v]
+            if True:
+                bank = new_bank("row_bank", [P, HALF])
+                row_banks[v] = bank
+                for b in range(BLOCKS):
+                    nc.tensor.transpose(
+                        bank[:, P * b : P * (b + 1)], col[:, b : b + 1].to_broadcast([P, P]), ident[:]
+                    )
 
-        def solver_group(h):
-            src = solver_raw[h][:].rearrange("p j n -> p n j")
-            if h == 0:
-                nc.scalar.copy(out=solver_grp[h][:], in_=src)
+        def store_row(v, engine_copy):
+            engine_copy(out=(raised_bias_row, travel_row, floor_row)[v][:], in_=row_banks[v][:])
+
+        def group_solver(h, on_scalar):
+            source = solver_raw[h][:].rearrange("p t n -> p n t")
+            if on_scalar:
+                nc.scalar.copy(out=solver_grouped[h][:], in_=source)
             else:
-                nc.vector.tensor_copy(out=solver_grp[h][:], in_=src)
+                nc.vector.tensor_copy(out=solver_grouped[h][:], in_=source)
 
-        def solver_quantize(h):
+        def quantize_solver(h):
             nc.vector.quantize_mx(
                 out=solver_codes[h][:].bitcast(FP8X4),
-                scales=solver_sc[h][:],
-                in_=solver_grp[h][:].rearrange("p n j -> p (n j)"),
+                scales=solver_scales[h][:],
+                in_=solver_grouped[h][:].rearrange("p n t -> p (n t)"),
             )
 
         grouped, split = {}, {}
 
-        def head_turn(j):
-            new = work.tile([P, PASSES, P, 4], BF16, name="grouped_h", tag="grouped", bufs=4, align_bytes=64)
-            grouped["h", j] = new
-            pairs = head_raw[j][:].bitcast(F32)
-            gw = new[:].rearrange("p c r t -> p (c r t)").bitcast(F32).rearrange(
+        def turn_tile(j):
+            new = work.tile([P, PASSES, P, 4], BF16, name="grouped_tile", tag="grouped", bufs=3, align_bytes=64)
+            grouped["tile", j] = new
+            pairs = tile_raw[j][:].bitcast(F32)
+            by_pair = new[:].rearrange("p c r t -> p (c r t)").bitcast(F32).rearrange(
                 "p (c r u) -> p c r u", c=PASSES, u=2
             )
-            for b in range(2):
-                bank = psum.tile([P, 2, 2, P], F32, name="x_bank", tag="xt", bufs=XT)
-                for cc in range(2):
+            for c0 in (0, 2):
+                bank = turn_bank("tile_bank", [P, 2, 2, P])
+                for c in (0, 1):
+                    first = KP // 2 * (c0 + c)
                     for u in range(2):
-                        base = 256 * (2 * b + cc)
-                        nc.tensor.transpose(bank[:, cc, u, :], pairs[:, base + u : base + 256 : 2], ident[:])
-                nc.scalar.copy(out=gw[:, 2 * b : 2 * b + 2, :, :], in_=bank[:].rearrange("p c u r -> p c r u"))
+                        nc.tensor.transpose(bank[:, c, u, :], pairs[:, first + u : first + KP // 2 : 2], ident[:])
+                nc.scalar.copy(out=by_pair[:, c0 : c0 + 2, :, :], in_=bank[:].rearrange("p c u r -> p c r u"))
 
-        def head_quantize(j):
-            for c in range(PASSES):
+        def quantize_tile(j, passes=range(PASSES)):
+            frames_j = slice(P * j, P * (j + 1))
+            for c in passes:
                 nc.vector.quantize_mx(
-                    out=codes[0][:, c, P * j : P * (j + 1)].bitcast(FP8X4),
-                    scales=scales[0][:, c, P * j : P * (j + 1)],
-                    in_=grouped["h", j][:, c, :, :].rearrange("p r t -> p (r t)"),
+                    out=codes[0][:, c, frames_j].bitcast(FP8X4),
+                    scales=scales[0][:, c, frames_j],
+                    in_=grouped["tile", j][:, c, :, :].rearrange("p r t -> p (r t)"),
                 )
 
-        def unit_split(n):
+        def split_pass(n):
             new = work.tile([P, TILES, 2, P], F32, name="split", bufs=2, align_bytes=64)
             split[n] = new
             nc.vector.tensor_copy(
-                out=new[:],
-                in_=raw[n // 4 + 1, n % 4][:].bitcast(F32).rearrange("p j (m u) -> p j u m", u=2),
+                out=new[:], in_=pass_raw[n][:].bitcast(F32).rearrange("p j (m u) -> p j u m", u=2)
             )
 
-        def unit_turn(n):
-            words_of = raw[n // 4 + 1, n % 4][:].bitcast(F32)
-            new = work.tile([P, TILES, P, 4], BF16, name="grouped_u", tag="grouped", bufs=4, align_bytes=64)
-            grouped[n] = new
-            gw = new[:].rearrange("p j r t -> p (j r t)").bitcast(F32).rearrange(
+        def turn_pass(n):
+            new = work.tile([P, TILES, P, 4], BF16, name="grouped_pass", tag="grouped", bufs=3, align_bytes=64)
+            grouped["pass", n] = new
+            pairs = pass_raw[n][:].bitcast(F32)
+            by_pair = new[:].rearrange("p j r t -> p (j r t)").bitcast(F32).rearrange(
                 "p (j r u) -> p j r u", j=TILES, u=2
             )
-            for b in range(2):
-                bank = psum.tile([P, 2, 2, P], F32, name="x_bank", tag="xt", bufs=XT)
-                for jj in range(2):
+            for j0 in (0, 2):
+                bank = turn_bank("pass_bank", [P, 2, 2, P])
+                for j in (0, 1):
                     for u in range(2):
-                        src = split[n][:, 2 * b + jj, u, :] if n in split else words_of[:, 2 * b + jj, u : 256 : 2]
-                        nc.tensor.transpose(bank[:, jj, u, :], src, ident[:])
-                nc.scalar.copy(out=gw[:, 2 * b : 2 * b + 2, :, :], in_=bank[:].rearrange("p j u r -> p j r u"))
+                        source = split[n][:, j0 + j, u, :] if n in split else pairs[:, j0 + j, u : KP // 2 : 2]
+                        nc.tensor.transpose(bank[:, j, u, :], source, ident[:])
+                nc.scalar.copy(out=by_pair[:, j0 : j0 + 2, :, :], in_=bank[:].rearrange("p j u r -> p j r u"))
 
-        def unit_quantize(n):
-            g, c = n // 4 + 1, n % 4
+        def quantize_pass(n):
+            g, c = n // PASSES + 1, n % PASSES
             nc.vector.quantize_mx(
                 out=codes[g][:, c, :].bitcast(FP8X4),
                 scales=scales[g][:, c, :],
-                in_=grouped[n][:].rearrange("p j r t -> p (j r t)"),
+                in_=grouped["pass", n][:].rearrange("p j r t -> p (j r t)"),
             )
 
-        def weight(c, h, c0, c1):
+        def solver_operand(c, h, first, last):
             if c < SKIN_PASSES:
-                base = N * c + HALF * h
-                return words[h][:, c, 2 * c0 : 2 * c1].bitcast(FP4X4), skin_sc[:, base + c0 : base + c1]
-            return solver_codes[h][:, c0:c1].bitcast(FP8X4), solver_sc[h][:, c0:c1]
+                column = N * c + HALF * h
+                return words[h][:, c, 2 * first : 2 * last].bitcast(FP4X4), word_scales[:, column + first : column + last]
+            return solver_codes[h][:, first:last].bitcast(FP8X4), solver_scales[h][:, first:last]
 
-        def frames(g, c, t0, t1):
-            return codes[g][:, c, t0:t1].bitcast(FP8X4), scales[g][:, c, t0:t1]
+        def frame_operand(g, c, first, last):
+            return codes[g][:, c, first:last].bitcast(FP8X4), scales[g][:, c, first:last]
 
-        def product(acc, lhs, rhs, c):
+        def multiply(acc, c, stationary, moving):
             nc.tensor.matmul_mx(
-                out=acc[:], lhsT=lhs[0], lhsT_scale=lhs[1], rhs=rhs[0], rhs_scale=rhs[1],
-                start=(c == 0), stop=(c == PASSES - 1),
+                out=acc,
+                lhsT=stationary[0],
+                lhsT_scale=stationary[1],
+                rhs=moving[0],
+                rhs_scale=moving[1],
+                start=(c == 0),
+                stop=(c == PASSES - 1),
             )
 
-        acc_t, acc_c, xs, ys, zs, as_, vs, o_c = {}, {}, {}, {}, {}, {}, {}, {}
+        f_acc, f_raised, f_relu, f_moved = {}, {}, {}, {}
 
-        def t_mm(i, passes=range(PASSES)):
+        def f_product(i, passes=range(PASSES)):
+            g, j = divmod(i, TILES)
             if passes[0] == 0:
-                new = psum.tile([P, 512], F32, name="acc_t", tag="acc", bufs=ACC)
-                acc_t[i] = new
-            g, j = i // 4, i % 4
+                new = acc_bank("f_acc")
+                f_acc[i] = new
             for c in passes:
-                product(acc_t[i], frames(g, c, P * j, P * (j + 1)), weight(c, 0, 0, HALF), c)
+                multiply(f_acc[i][:], c, frame_operand(g, c, P * j, P * (j + 1)), solver_operand(c, 0, 0, HALF))
 
-        def t_bias(i):
-            new = work.tile([P, HALF], F32, name="x", bufs=4, align_bytes=64)
-            xs[i] = new
-            nc.vector.tensor_tensor(out=new[:], in0=acc_t[i][:], in1=bias_row[:], op=ALU.add)
+        def f_add_bias(i):
+            new = work.tile([P, HALF], F32, name="f_raised", align_bytes=64)
+            f_raised[i] = new
+            nc.vector.tensor_tensor(out=new[:], in0=f_acc[i][:], in1=raised_bias_row[:], op=ALU.add)
 
-        def t_relu(i):
-            new = work.tile([P, HALF], F32, name="y", bufs=4, align_bytes=64)
-            ys[i] = new
-            nc.scalar.activation(out=new[:], in_=xs[i][:], func=ACT.Relu)
+        def f_clamp_low(i):
+            new = work.tile([P, HALF], F32, name="f_relu", align_bytes=64)
+            f_relu[i] = new
+            nc.scalar.activation(out=new[:], in_=f_raised[i][:], func=ACT.Relu)
 
-        def t_scale(i):
-            new = work.tile([P, HALF], F32, name="z", bufs=4, align_bytes=64)
-            zs[i] = new
+        def f_clamp_high_and_scale(i):
+            new = work.tile([P, HALF], F32, name="f_moved", align_bytes=64)
+            f_moved[i] = new
             nc.vector.scalar_tensor_tensor(
-                out=new[:], in0=ys[i][:], scalar=W_HIGH - W_LOW, in1=travel_row[:], op0=ALU.min, op1=ALU.mult
+                out=new[:], in0=f_relu[i][:], scalar=W_HIGH - W_LOW, in1=travel_row[:], op0=ALU.min, op1=ALU.mult
             )
 
-        def t_rest(i):
-            o = work.tile([P, HALF], F32, name="o", bufs=6, align_bytes=64)
-            nc.vector.tensor_tensor(out=o[:], in0=zs[i][:], in1=rest_row[:], op=ALU.add)
-            nc.sync.dma_start(out=group_rows(out, i // 4)[:, i % 4, 0:HALF], in_=o[:])
+        def f_finish(i):
+            g, j = divmod(i, TILES)
+            result = work.tile([P, HALF], F32, name="f_result", tag="result", bufs=6, align_bytes=64)
+            nc.vector.tensor_tensor(out=result[:], in0=f_moved[i][:], in1=floor_row[:], op=ALU.add)
+            nc.sync.dma_start(out=group_rows(out, g)[:, j, 0:HALF], in_=result[:])
 
-        def c_mm(i):
-            new = psum.tile([P, 512], F32, name="acc_c", tag="acc", bufs=ACC)
-            acc_c[i] = new
-            g, b = i // 4, i % 4
+        c_acc, c_affine, c_clamped, c_turned, c_pair = {}, {}, {}, {}, {}
+
+        def c_column(i):
+            return slice(BLOCKS + i % BLOCKS, BLOCKS + i % BLOCKS + 1)
+
+        def c_product(i):
+            g, b = divmod(i, BLOCKS)
+            new = acc_bank("c_acc")
+            c_acc[i] = new
             for c in range(PASSES):
-                product(new, weight(c, 1, P * b, P * (b + 1)), frames(g, c, 0, GROUP), c)
+                multiply(new[:], c, solver_operand(c, 1, P * b, P * (b + 1)), frame_operand(g, c, 0, GROUP))
 
-        def c_affine(i):
-            new = work.tile([P, GROUP], F32, name="a", bufs=4, align_bytes=64)
-            as_[i] = new
-            k = BLOCKS + i % 4
+        def c_scale_and_shift(i, acc, width):
+            new = work.tile([P, width], F32, name="c_affine", align_bytes=64)
             nc.scalar.activation(
-                out=new[:], in_=acc_c[i][:], func=ACT.Identity, bias=shift[:, k : k + 1], scale=cols[:, 8 + k : 9 + k]
+                out=new[:], in_=acc, func=ACT.Identity, bias=shift_col[:, c_column(i)], scale=travel_col[:, c_column(i)]
             )
+            return new
 
-        def c_clamp(i):
-            new = work.tile([P, GROUP], F32, name="v", bufs=4, align_bytes=64)
-            vs[i] = new
-            k = BLOCKS + i % 4
+        def c_clamp(i, affine, width):
+            new = work.tile([P, width], F32, name="c_clamped", bufs=4, align_bytes=64)
             nc.vector.tensor_scalar(
-                out=new[:], in0=as_[i][:], scalar1=low[:, k : k + 1], scalar2=high[:, k : k + 1],
-                op0=ALU.max, op1=ALU.min,
+                out=new[:],
+                in0=affine[:],
+                scalar1=low_col[:, c_column(i)],
+                scalar2=high_col[:, c_column(i)],
+                op0=ALU.max,
+                op1=ALU.min,
             )
+            return new
 
-        def c_back(i):
-            g, b = i // 4, i % 4
-            bank = psum.tile([P, TILES, P], F32, name="back", tag="back", bufs=BACK)
-            acc_c[i] = bank
-            for j in range(TILES):
-                nc.tensor.transpose(bank[:, j, :], vs[i][:, P * j : P * (j + 1)], ident[:])
-
-        def c_out(i):
-            g, b = i // 4, i % 4
-            if b % 2 == 0:
-                new = work.tile([P, TILES, 2, P], F32, name="o_c", bufs=4, align_bytes=64)
-                o_c[i // 2] = new
-            pair = o_c[i // 2]
-            nc.scalar.copy(out=pair[:, :, b % 2, :], in_=acc_c[i][:])
-            if b % 2 == 1:
-                nc.sync.dma_start(
-                    out=group_rows(out, g)[:, :, HALF + P * (b - 1) : HALF + P * (b + 1)],
-                    in_=pair[:].rearrange("p j b n -> p j (b n)"),
-                )
-
-        def last_c():
-            i = 15
-            g, b, k = 3, 3, BLOCKS + 3
-            accs, ys_, banks = [], [], []
-            for e in range(2):
-                acc = psum.tile([P, 2, P], F32, name=f"acc_l{e}", tag="xt", bufs=XT)
-                accs.append(acc)
-                for jj in range(2):
-                    t0 = P * (2 * e + jj)
-                    for c in range(PASSES):
-                        lhs, rhs = weight(c, 1, P * b, P * (b + 1)), frames(g, c, t0, t0 + P)
-                        nc.tensor.matmul_mx(
-                            out=acc[:, jj, :], lhsT=lhs[0], lhsT_scale=lhs[1], rhs=rhs[0], rhs_scale=rhs[1],
-                            start=(c == 0), stop=(c == PASSES - 1),
-                        )
-            return accs
-
-        def last_affine(accs, e):
-            k = BLOCKS + 3
-            a = work.tile([P, 2 * P], F32, name=f"a_l{e}", tag="a", bufs=4, align_bytes=64)
-            nc.scalar.activation(
-                out=a[:], in_=accs[e][:].rearrange("p j r -> p (j r)"), func=ACT.Identity,
-                bias=shift[:, k : k + 1], scale=cols[:, 8 + k : 9 + k],
-            )
-            return a
-
-        def last_clamp(a, e):
-            k = BLOCKS + 3
-            v = work.tile([P, 2 * P], F32, name=f"v_l{e}", tag="v", bufs=4, align_bytes=64)
-            nc.vector.tensor_scalar(
-                out=v[:], in0=a[:], scalar1=low[:, k : k + 1], scalar2=high[:, k : k + 1], op0=ALU.max, op1=ALU.min
-            )
-            return v
-
-        def last_back(v, e):
-            bank = psum.tile([P, 2, P], F32, name=f"back_l{e}", tag="back", bufs=BACK)
-            for jj in range(2):
-                nc.tensor.transpose(bank[:, jj, :], v[:, P * jj : P * (jj + 1)], ident[:])
+        def c_turn_back(clamped, tiles):
+            bank = back_bank("back_bank", [P, tiles, P])
+            for j in range(tiles):
+                nc.tensor.transpose(bank[:, j, :], clamped[:, P * j : P * (j + 1)], ident[:])
             return bank
 
-        def last_out(bank, e):
-            o = work.tile([P, 2, P], F32, name=f"o_l{e}", tag="o", bufs=6, align_bytes=64)
-            eng = nc.scalar.copy if e else nc.vector.tensor_copy
-            eng(out=o[:], in_=bank[:])
-            nc.sync.dma_start(out=group_rows(out, 3)[:, 2 * e : 2 * e + 2, HALF + 3 * P : N], in_=o[:])
+        def c_finish(i, bank):
+            g, b = divmod(i, BLOCKS)
+            if b % 2 == 0:
+                new = work.tile([P, TILES, 2, P], F32, name="c_pair", align_bytes=64)
+                c_pair[i // 2] = new
+            pair = c_pair[i // 2]
+            nc.scalar.copy(out=pair[:, :, b % 2, :], in_=bank[:])
+            if b % 2 == 1:
+                first = HALF + P * (b - 1)
+                nc.sync.dma_start(
+                    out=group_rows(out, g)[:, :, first : first + 2 * P], in_=pair[:].rearrange("p j b n -> p j (b n)")
+                )
 
-        def c_out_single(i):
-            o = work.tile([P, TILES, P], F32, name="o_s", tag="o", bufs=6, align_bytes=64)
-            nc.scalar.copy(out=o[:], in_=acc_c[i][:])
-            nc.sync.dma_start(out=group_rows(out, 3)[:, :, HALF + 2 * P : HALF + 3 * P], in_=o[:])
+        def c_return(i):
+            c_finish(i, c_turn_back(c_clamped[i], TILES))
 
-        with tc.manual_schedule():
-            head_turn(0)
-            vectors_to_columns()
-            head_quantize(0)
-            solver_group(0)
-            bb = column_to_row(bias_row, bias_up[:])
-            tb = column_to_row(travel_row, t_col)
-            rb = column_to_row(rest_row, rest_low[:], "acc", 4)
-            row_copy(bias_row, bb)
-            row_copy(travel_row, tb)
-            row_copy(rest_row, rb)
-            t_mm(0, range(3))
-            head_turn(1)
-            solver_quantize(0)
-            t_mm(0, range(3, 4))
-            solver_group(1)
-            head_quantize(1)
-            t_bias(0)
-            head_turn(2)
-            t_relu(0)
-            t_mm(1)
-            solver_quantize(1)
-            head_quantize(2)
-            t_bias(1)
-            t_scale(0)
-            head_turn(3)
-            t_relu(1)
-            t_mm(2)
-            t_rest(0)
-            head_quantize(3)
-            t_bias(2)
-            t_scale(1)
-            t_relu(2)
-            unit_split(1)
-            unit_turn(0)
-            t_mm(3)
-            t_bias(3)
-            t_relu(3)
-            unit_quantize(0)
-            unit_split(2)
-            t_rest(1)
-            t_scale(2)
-            c_mm(0)
-            unit_turn(1)
-            c_affine(0)
-            c_mm(1)
-            c_clamp(0)
-            unit_quantize(1)
-            c_affine(1)
-            unit_split(3)
-            t_rest(2)
-            unit_turn(2)
-            c_back(0)
-            c_out(0)
-            c_mm(2)
-            c_clamp(1)
-            unit_quantize(2)
-            t_scale(3)
-            c_affine(2)
-            unit_turn(3)
-            c_back(1)
-            c_out(1)
-            c_mm(3)
-            c_clamp(2)
-            unit_split(4)
-            unit_quantize(3)
-            t_rest(3)
-            for i in range(4, 16):
-                c_affine(i - 1)
-                if i > 4:
-                    t_bias(i - 1)
-                if i > 5:
-                    t_rest(i - 2)
-                if i < 12:
-                    unit_turn(i)
-                if i + 1 < 12:
-                    unit_split(i + 1)
-                c_clamp(i - 1)
-                c_back(i - 2)
-                if i > 4:
-                    t_relu(i - 1)
-                c_out(i - 2)
-                if i < 12:
-                    unit_quantize(i)
-                if i > 4:
-                    t_scale(i - 1)
-                t_mm(i)
-                if i < 15:
-                    c_mm(i)
-            accs = last_c()
-            t_bias(15)
-            t_relu(15)
-            t_rest(14)
-            c_back(14)
-            a0 = last_affine(accs, 0)
-            t_scale(15)
-            a1 = last_affine(accs, 1)
-            v0 = last_clamp(a0, 0)
-            c_out_single(14)
-            v1 = last_clamp(a1, 1)
-            t_rest(15)
-            b0 = last_back(v0, 0)
-            b1 = last_back(v1, 1)
-            last_out(b0, 0)
-            last_out(b1, 1)
+        def c_scale(i):
+            c_affine[i] = c_scale_and_shift(i, c_acc[i][:], GROUP)
 
+        def c_limit(i):
+            c_clamped[i] = c_clamp(i, c_affine[i], GROUP)
 
-XT, ACC, BACK = 2, 4, 2
+        END = UNITS - 1
+
+        def end_store(bank, engine_copy, i, j0, tiles):
+            first = HALF + P * (i % BLOCKS)
+            result = work.tile([P, tiles, P], F32, name="end_result", tag="result", bufs=6, align_bytes=64)
+            engine_copy(out=result[:], in_=bank[:])
+            nc.sync.dma_start(out=group_rows(out, GROUPS - 1)[:, j0 : j0 + tiles, first : first + P], in_=result[:])
+
+        def end_product(half):
+            b = END % BLOCKS
+            acc = turn_bank("end_acc", [P, 2, P])
+            for j in range(2):
+                first = P * (2 * half + j)
+                for c in range(PASSES):
+                    multiply(
+                        acc[:, j, :],
+                        c,
+                        solver_operand(c, 1, P * b, P * (b + 1)),
+                        frame_operand(GROUPS - 1, c, first, first + P),
+                    )
+            return acc[:].rearrange("p j r -> p (j r)")
+
+        warm_quant()
+        turn_tile(0)
+        warm_up(14)
+        group_solver(0, False)
+        widen_vectors()
+        quantize_solver(0)
+        quantize_tile(0, (0, 1))
+        quantize_tile(0, (2, 3))
+        f_product(0, range(SKIN_PASSES))
+        turn_vectors()
+        turn_tile(1)
+        derive_columns()
+        warm_up(8)
+        f_product(0, range(SKIN_PASSES, PASSES))
+        turn_row(0, back_bank)
+        turn_row(1, back_bank)
+        quantize_tile(1, (0, 1))
+        turn_tile(2)
+        quantize_tile(1, (2, 3))
+        store_row(0, nc.vector.tensor_copy)
+        group_solver(1, False)
+        f_product(1)
+        turn_tile(3)
+        store_row(1, nc.vector.tensor_copy)
+        turn_row(2, back_bank)
+        quantize_tile(2, (0, 1))
+        f_add_bias(1)
+        f_clamp_low(1)
+        quantize_tile(2, (2, 3))
+        f_add_bias(0)
+        f_clamp_low(0)
+        split_pass(1)
+        store_row(2, nc.scalar.copy)
+        quantize_tile(3, (2, 3))
+        quantize_solver(1)
+        f_product(2)
+        turn_pass(0)
+        quantize_tile(3, (0, 1))
+        f_clamp_high_and_scale(0)
+        f_clamp_high_and_scale(1)
+        f_add_bias(2)
+        f_product(3)
+        f_add_bias(3)
+        f_clamp_low(2)
+        turn_pass(1)
+        split_pass(2)
+        c_product(0)
+        c_scale(0)
+        f_clamp_low(3)
+        split_pass(3)
+        c_product(1)
+        c_scale(1)
+        f_finish(0)
+        quantize_pass(0)
+        f_clamp_high_and_scale(2)
+        turn_pass(2)
+        c_product(2)
+        f_clamp_high_and_scale(3)
+        c_limit(1)
+        c_limit(0)
+        f_finish(2)
+        quantize_pass(2)
+        quantize_pass(1)
+        turn_pass(3)
+        c_scale(2)
+        split_pass(4)
+        f_finish(1)
+        c_limit(2)
+        c_return(0)
+        c_return(1)
+        quantize_pass(3)
+        c_product(3)
+        f_finish(3)
+        for i in range(4, UNITS):
+            c_scale(i - 1)
+            if i > 4:
+                f_add_bias(i - 1)
+            if i > 5:
+                f_finish(i - 2)
+            if i < UNITS - TILES:
+                turn_pass(i)
+            if i + 1 < UNITS - TILES:
+                split_pass(i + 1)
+            c_limit(i - 1)
+            bank = c_turn_back(c_clamped[i - 2], TILES)
+            if i > 4:
+                f_clamp_low(i - 1)
+            c_finish(i - 2, bank)
+            if i < UNITS - TILES:
+                quantize_pass(i)
+            if i > 4:
+                f_clamp_high_and_scale(i - 1)
+            f_product(i)
+            if i < END:
+                c_product(i)
+
+        acc_0 = end_product(0)
+        acc_1 = end_product(1)
+        f_add_bias(END)
+        f_clamp_low(END)
+        f_finish(END - 1)
+        bank = c_turn_back(c_clamped[END - 1], TILES)
+        affine_0 = c_scale_and_shift(END, acc_0, GROUP // 2)
+        f_clamp_high_and_scale(END)
+        affine_1 = c_scale_and_shift(END, acc_1, GROUP // 2)
+        clamped_0 = c_clamp(END, affine_0, GROUP // 2)
+        end_store(bank, nc.scalar.copy, END - 1, 0, TILES)
+        clamped_1 = c_clamp(END, affine_1, GROUP // 2)
+        f_finish(END)
+        back_0 = c_turn_back(clamped_0, 2)
+        back_1 = c_turn_back(clamped_1, 2)
+        end_store(back_0, nc.vector.tensor_copy, END, 0, 2)
+        end_store(back_1, nc.scalar.copy, END, 2, 2)

@@ -27,6 +27,7 @@ HALF = N // 2
 BLOCKS = HALF // P
 UNITS = GROUPS * TILES
 W_LOW, W_HIGH = -0.5, 1.0
+SPLIT_BUFS = 3
 TURN_BANKS, ACC_BANKS = 2, 4
 
 
@@ -184,11 +185,12 @@ def tile_face_retarget_rig_s1_kernel(
             engine_copy(out=(raised_bias_row, travel_row, floor_row)[v][:], in_=row_banks[v][:])
 
         def group_solver(h, on_scalar):
-            source = solver_raw[h][:].rearrange("p t n -> p n t")
+            source = solver_raw[h][:].rearrange("p t (c i) -> p c t i", i=4)
+            target = solver_grouped[h][:].rearrange("p (c i) t -> p c t i", i=4)
             if on_scalar:
-                nc.scalar.copy(out=solver_grouped[h][:], in_=source)
+                nc.scalar.copy(out=target, in_=source)
             else:
-                nc.vector.tensor_copy(out=solver_grouped[h][:], in_=source)
+                nc.vector.tensor_copy(out=target, in_=source)
 
         def quantize_solver(h):
             nc.vector.quantize_mx(
@@ -198,6 +200,13 @@ def tile_face_retarget_rig_s1_kernel(
             )
 
         grouped, split = {}, {}
+
+        def split_tile(j):
+            new = work.tile([P, PASSES, 2, P], F32, name="split_tile", tag="split", bufs=SPLIT_BUFS, align_bytes=64)
+            split["tile", j] = new
+            nc.vector.tensor_copy(
+                out=new[:], in_=tile_raw[j][:].bitcast(F32).rearrange("p (c m u) -> p c u m", c=PASSES, u=2)
+            )
 
         def turn_tile(j):
             new = work.tile([P, PASSES, P, 4], BF16, name="grouped_tile", tag="grouped", bufs=3, align_bytes=64)
@@ -211,7 +220,8 @@ def tile_face_retarget_rig_s1_kernel(
                 for c in (0, 1):
                     first = KP // 2 * (c0 + c)
                     for u in range(2):
-                        nc.tensor.transpose(bank[:, c, u, :], pairs[:, first + u : first + KP // 2 : 2], ident[:])
+                        source = split["tile", j][:, c0 + c, u, :] if ("tile", j) in split else pairs[:, first + u : first + KP // 2 : 2]
+                        nc.tensor.transpose(bank[:, c, u, :], source, ident[:])
                 nc.scalar.copy(out=by_pair[:, c0 : c0 + 2, :, :], in_=bank[:].rearrange("p c u r -> p c r u"))
 
         def quantize_tile(j, passes=range(PASSES)):
@@ -224,7 +234,7 @@ def tile_face_retarget_rig_s1_kernel(
                 )
 
         def split_pass(n):
-            new = work.tile([P, TILES, 2, P], F32, name="split", bufs=2, align_bytes=64)
+            new = work.tile([P, TILES, 2, P], F32, name="split", tag="split", bufs=SPLIT_BUFS, align_bytes=64)
             split[n] = new
             nc.vector.tensor_copy(
                 out=new[:], in_=pass_raw[n][:].bitcast(F32).rearrange("p j (m u) -> p j u m", u=2)
@@ -387,116 +397,161 @@ def tile_face_retarget_rig_s1_kernel(
                     )
             return acc[:].rearrange("p j r -> p (j r)")
 
-        warm_quant()
+        done = set()
+        c_bank = {}
+
+        def c_back(i):
+            c_bank[i] = c_turn_back(c_clamped[i], TILES)
+
+        def c_store(i):
+            c_finish(i, c_bank[i])
+
+        RANGES = {
+            split_pass: (1, 12), turn_pass: (0, 12), quantize_pass: (0, 12),
+            f_product: (1, 16), f_add_bias: (0, 16), f_clamp_low: (0, 16), f_clamp_high_and_scale: (0, 16), f_finish: (0, 16),
+            c_product: (0, 15), c_scale: (0, 15), c_limit: (0, 15), c_back: (0, 15), c_store: (0, 14),
+        }
+
+        def once(op, n):
+            if (op, n) in done or not RANGES[op][0] <= n < RANGES[op][1]:
+                return
+            done.add((op, n))
+            op(n)
+
         turn_tile(0)
-        warm_up(14)
-        group_solver(0, False)
-        widen_vectors()
-        quantize_solver(0)
+        warm_quant()
         quantize_tile(0, (0, 1))
+        warm_up(2)
+        group_solver(0, True)
         quantize_tile(0, (2, 3))
         f_product(0, range(SKIN_PASSES))
+        widen_vectors()
         turn_vectors()
-        turn_tile(1)
         derive_columns()
-        warm_up(8)
-        f_product(0, range(SKIN_PASSES, PASSES))
-        turn_row(0, back_bank)
-        turn_row(1, back_bank)
-        quantize_tile(1, (0, 1))
-        turn_tile(2)
-        quantize_tile(1, (2, 3))
-        store_row(0, nc.vector.tensor_copy)
+        turn_tile(1)
+        quantize_solver(0)
         group_solver(1, False)
-        f_product(1)
-        turn_tile(3)
-        store_row(1, nc.vector.tensor_copy)
+        quantize_tile(1, (0, 1))
+        quantize_tile(1, (2, 3))
+        split_tile(3)
+        warm_up(4)
+        turn_row(0, back_bank)
+        turn_tile(2)
+        f_product(0, range(SKIN_PASSES, PASSES))
+        quantize_solver(1)
+        once(f_product, 1)
+        turn_row(1, back_bank)
+        store_row(0, nc.scalar.copy)
         turn_row(2, back_bank)
         quantize_tile(2, (0, 1))
-        f_add_bias(1)
-        f_clamp_low(1)
+        once(f_add_bias, 0)
+        once(f_add_bias, 1)
         quantize_tile(2, (2, 3))
-        f_add_bias(0)
-        f_clamp_low(0)
-        split_pass(1)
-        store_row(2, nc.scalar.copy)
-        quantize_tile(3, (2, 3))
-        quantize_solver(1)
-        f_product(2)
-        turn_pass(0)
+        turn_tile(3)
+        once(f_clamp_low, 1)
         quantize_tile(3, (0, 1))
-        f_clamp_high_and_scale(0)
-        f_clamp_high_and_scale(1)
-        f_add_bias(2)
-        f_product(3)
-        f_add_bias(3)
-        f_clamp_low(2)
-        turn_pass(1)
-        split_pass(2)
-        c_product(0)
-        c_scale(0)
-        f_clamp_low(3)
-        split_pass(3)
-        c_product(1)
-        c_scale(1)
-        f_finish(0)
-        quantize_pass(0)
-        f_clamp_high_and_scale(2)
-        turn_pass(2)
-        c_product(2)
-        f_clamp_high_and_scale(3)
-        c_limit(1)
-        c_limit(0)
-        f_finish(2)
-        quantize_pass(2)
-        quantize_pass(1)
-        turn_pass(3)
-        c_scale(2)
-        split_pass(4)
-        f_finish(1)
-        c_limit(2)
-        c_return(0)
-        c_return(1)
-        quantize_pass(3)
-        c_product(3)
-        f_finish(3)
-        for i in range(4, UNITS):
-            c_scale(i - 1)
-            if i > 4:
-                f_add_bias(i - 1)
-            if i > 5:
-                f_finish(i - 2)
-            if i < UNITS - TILES:
-                turn_pass(i)
-            if i + 1 < UNITS - TILES:
-                split_pass(i + 1)
-            c_limit(i - 1)
-            bank = c_turn_back(c_clamped[i - 2], TILES)
-            if i > 4:
-                f_clamp_low(i - 1)
-            c_finish(i - 2, bank)
-            if i < UNITS - TILES:
-                quantize_pass(i)
-            if i > 4:
-                f_clamp_high_and_scale(i - 1)
-            f_product(i)
-            if i < END:
-                c_product(i)
-
+        quantize_tile(3, (2, 3))
+        once(f_product, 2)
+        store_row(1, nc.vector.tensor_copy)
+        once(f_clamp_low, 0)
+        once(split_pass, 1)
+        once(turn_pass, 0)
+        once(split_pass, 2)
+        store_row(2, nc.vector.tensor_copy)
+        once(f_clamp_high_and_scale, 1)
+        once(c_product, 0)
+        once(f_add_bias, 2)
+        once(split_pass, 3)
+        once(c_scale, 0)
+        once(f_clamp_low, 2)
+        once(turn_pass, 1)
+        once(f_product, 3)
+        once(c_product, 1)
+        once(f_clamp_high_and_scale, 2)
+        once(c_scale, 1)
+        once(f_add_bias, 3)
+        once(turn_pass, 2)
+        once(c_limit, 0)
+        once(f_finish, 1)
+        once(c_limit, 1)
+        once(quantize_pass, 0)
+        once(f_clamp_high_and_scale, 0)
+        once(c_product, 2)
+        once(c_scale, 2)
+        once(turn_pass, 3)
+        once(c_back, 0)
+        once(quantize_pass, 1)
+        once(split_pass, 4)
+        once(c_back, 1)
+        once(f_finish, 0)
+        once(quantize_pass, 2)
+        once(c_limit, 2)
+        once(c_product, 3)
+        once(c_store, 0)
+        once(quantize_pass, 3)
+        once(f_finish, 2)
+        once(c_scale, 3)
+        once(split_pass, 5)
+        once(c_store, 1)
+        for i in range(4, UNITS, 2):
+            once(c_limit, i + -1)
+            once(turn_pass, i + 0)
+            once(f_product, i + 0)
+            once(f_add_bias, i + 0)
+            once(f_clamp_low, i + -1)
+            once(f_clamp_low, i + 0)
+            once(c_product, i + 0)
+            once(c_back, i + -2)
+            once(c_store, i + -2)
+            once(f_clamp_high_and_scale, i + -1)
+            once(split_pass, i + 2)
+            once(c_back, i + -1)
+            once(c_store, i + -1)
+            once(f_clamp_high_and_scale, i + 0)
+            once(quantize_pass, i + 0)
+            once(split_pass, i + 3)
+            once(turn_pass, i + 1)
+            once(f_product, i + 1)
+            once(quantize_pass, i + 1)
+            once(c_product, i + 1)
+            once(f_finish, i + -1)
+            once(f_add_bias, i + 1)
+            once(c_scale, i + 0)
+            once(c_limit, i + 0)
+            once(f_finish, i + 0)
+            once(c_scale, i + 1)
+        once(f_add_bias, 14)
         acc_0 = end_product(0)
-        acc_1 = end_product(1)
-        f_add_bias(END)
-        f_clamp_low(END)
-        f_finish(END - 1)
-        bank = c_turn_back(c_clamped[END - 1], TILES)
         affine_0 = c_scale_and_shift(END, acc_0, GROUP // 2)
-        f_clamp_high_and_scale(END)
+        once(f_clamp_low, 14)
+        once(f_finish, 13)
+        once(c_scale, 14)
+        once(f_clamp_high_and_scale, 13)
+        once(c_back, 13)
+        acc_1 = end_product(1)
+        once(f_add_bias, 13)
+        once(f_clamp_low, 15)
+        once(c_scale, 13)
+        once(f_clamp_low, 13)
+        once(f_clamp_high_and_scale, 14)
+        once(c_back, 14)
+        once(f_finish, 12)
         affine_1 = c_scale_and_shift(END, acc_1, GROUP // 2)
         clamped_0 = c_clamp(END, affine_0, GROUP // 2)
-        end_store(bank, nc.scalar.copy, END - 1, 0, TILES)
-        clamped_1 = c_clamp(END, affine_1, GROUP // 2)
-        f_finish(END)
+        once(f_clamp_high_and_scale, 15)
         back_0 = c_turn_back(clamped_0, 2)
+        once(f_add_bias, 15)
+        clamped_1 = c_clamp(END, affine_1, GROUP // 2)
+        end_store(c_bank[14], nc.scalar.copy, END - 1, 0, TILES)
         back_1 = c_turn_back(clamped_1, 2)
-        end_store(back_0, nc.vector.tensor_copy, END, 0, 2)
+        once(c_store, 13)
+        once(c_back, 12)
+        once(c_limit, 13)
+        end_store(back_0, nc.scalar.copy, END, 0, 2)
+        once(f_finish, 15)
         end_store(back_1, nc.scalar.copy, END, 2, 2)
+        once(c_limit, 14)
+        once(f_finish, 14)
+        once(c_store, 12)
+        missing = [(0, n) for op in RANGES for n in range(RANGES[op][0], RANGES[op][1]) if (op, n) not in done]
+        assert not missing, missing

from contextlib import ExitStack

import concourse.mybir as mybir
from concourse.masks import make_identity

T, D, C, N = 2048, 1536, 512, 1024
FLOPS = 2 * T * (D + C) * N

F32 = mybir.dt.float32
BF16 = mybir.dt.bfloat16
I32 = mybir.dt.int32
U32 = mybir.dt.uint32
U8 = mybir.dt.uint8
FP8X4 = mybir.dt.float8_e4m3fn_x4
FP4X4 = mybir.dt.float4_e2m1fn_x4
ALU = mybir.AluOpType
ACT = mybir.ActivationFunctionType

P = 128
KP = 512
SKIN_PASSES = D // KP
PASSES = SKIN_PASSES + 1
GROUP = 512
GROUPS = T // GROUP
TILES = GROUP // P
HALF = N // 2
BLOCKS = HALF // P
UNITS = GROUPS * TILES
W_LOW, W_HIGH = -0.5, 1.0
SPLIT_BUFS = 3
TURN_BANKS, ACC_BANKS = 2, 4


def tile_face_retarget_rig_s1_kernel(
    tc, skin, skin_words, skin_scales, lips, lip_solver, actor_bias, travel, rest, out
):
    nc = tc.nc
    with ExitStack() as ctx:
        keep = ctx.enter_context(tc.tile_pool(name="keep", bufs=1))
        work = ctx.enter_context(tc.tile_pool(name="work", bufs=3))
        psum = ctx.enter_context(tc.psum_pool(name="psum", bufs=1))
        ctx.enter_context(tc.manual_schedule())

        def kept(name, shape, dtype):
            return keep.tile(shape, dtype, name=name, align_bytes=256)

        def turn_bank(name, shape):
            return psum.tile(shape, F32, name=name, tag="turn", bufs=TURN_BANKS)

        def back_bank(name, shape):
            return psum.tile(shape, F32, name=name, tag="back", bufs=2)

        def acc_bank(name, shape=(P, 512)):
            return psum.tile(list(shape), F32, name=name, tag="acc", bufs=ACC_BANKS)

        def group_rows(x, g):
            return x[GROUP * g : GROUP * (g + 1), :].rearrange("(p j) k -> p j k", j=TILES)

        ident = kept("ident", [P, P], F32)
        warm_in = kept("warm_in", [P, 4 * P], BF16)
        warm_codes = kept("warm_codes", [P, P], U32)
        warm_scales = kept("warm_scales", [P, P], U8)
        vec_rows = kept("vec_rows", [P, P], BF16)
        word_scales = kept("word_scales", [P, SKIN_PASSES * N], U8)
        words = [kept(f"words{h}", [P, SKIN_PASSES, 2 * HALF], U8) for h in range(2)]
        solver_raw = [kept(f"solver_raw{h}", [P, 4, HALF], BF16) for h in range(2)]
        solver_grouped = [kept(f"solver_grouped{h}", [P, HALF, 4], BF16) for h in range(2)]
        solver_codes = [kept(f"solver_codes{h}", [P, HALF], U32) for h in range(2)]
        solver_scales = [kept(f"solver_scales{h}", [P, HALF], U8) for h in range(2)]
        codes = [kept(f"codes{g}", [P, PASSES, GROUP], U32) for g in range(GROUPS)]
        scales = [kept(f"scales{g}", [P, PASSES, GROUP], U8) for g in range(GROUPS)]
        tile_raw = [kept(f"tile_raw{j}", [P, D + C], BF16) for j in range(TILES)]
        pass_raw = [kept(f"pass_raw{n}", [P, TILES, KP], BF16) for n in range((GROUPS - 1) * PASSES)]

        nc.vector.memset(warm_in[:], 1.0)
        for tile in (word_scales, vec_rows):
            nc.vector.memset(tile[:].bitcast(I32), 0)
        make_identity(nc, ident[:])

        def load_tile(j):
            nc.sync.dma_start(out=tile_raw[j][:, 0:D], in_=group_rows(skin, 0)[:, j, :])
            nc.sync.dma_start(out=tile_raw[j][:, D : D + C], in_=group_rows(lips, 0)[:, j, :])

        def load_words(h):
            by_row = skin_words.rearrange("g p n -> p g n")
            nc.sync.dma_start(out=words[h][:], in_=by_row[:, :, 2 * HALF * h : 2 * HALF * (h + 1)])

        def load_word_scales():
            dst = word_scales[:].bitcast(I32).rearrange("p (g n) -> p g n", g=SKIN_PASSES)
            src = skin_scales.bitcast(I32).rearrange("g q n -> q g n")
            for q in range(4):
                nc.scalar.dma_start(out=dst[32 * q : 32 * q + 4, :, :], in_=src[4 * q : 4 * q + 4, :, :])

        def load_solver(h):
            by_word = lip_solver.rearrange("(p t) n -> p t n", t=4)
            nc.sync.dma_start(out=solver_raw[h][:], in_=by_word[:, :, HALF * h : HALF * (h + 1)])

        def load_vectors():
            for v, vec in enumerate((actor_bias, travel, rest)):
                nc.gpsimd.dma_start(out=vec_rows[8 * v : 8 * v + 8, :], in_=vec.rearrange("(b n) -> b n", n=P))

        def load_pass(n):
            g, c = n // PASSES + 1, n % PASSES
            source = group_rows(skin, g)[:, :, KP * c : KP * (c + 1)] if c < SKIN_PASSES else group_rows(lips, g)
            nc.sync.dma_start(out=pass_raw[n][:], in_=source)

        load_word_scales()
        load_tile(0)
        load_vectors()
        load_words(0)
        load_solver(0)
        load_tile(1)
        load_solver(1)
        load_tile(2)
        load_tile(3)
        load_words(1)
        for n in range((GROUPS - 1) * PASSES):
            load_pass(n)

        cols = kept("cols", [P, 24], F32)
        bias_col, travel_col, rest_col = cols[:, 0:8], cols[:, 8:16], cols[:, 16:24]
        raised_bias_col = kept("raised_bias_col", [P, 8], F32)
        floor_col = kept("floor_col", [P, 8], F32)
        ceil_col = kept("ceil_col", [P, 8], F32)
        shift_col = kept("shift_col", [P, 8], F32)
        low_col = kept("low_col", [P, 8], F32)
        high_col = kept("high_col", [P, 8], F32)
        raised_bias_row = kept("raised_bias_row", [P, HALF], F32)
        travel_row = kept("travel_row", [P, HALF], F32)
        floor_row = kept("floor_row", [P, HALF], F32)

        def warm_quant():
            nc.vector.quantize_mx(out=warm_codes[:].bitcast(FP8X4), scales=warm_scales[:], in_=warm_in[:])

        def warm_up(count):
            bank = acc_bank("warm_bank")
            for i in range(count):
                nc.tensor.matmul_mx(
                    out=bank[:, 0:P],
                    lhsT=warm_codes[:].bitcast(FP8X4),
                    lhsT_scale=warm_scales[:],
                    rhs=warm_codes[:].bitcast(FP8X4),
                    rhs_scale=warm_scales[:],
                    start=True,
                    stop=True,
                )

        vec_f32 = kept("vec_f32", [P, P], F32)

        def widen_vectors():
            nc.vector.tensor_copy(out=vec_f32[:], in_=vec_rows[:])

        def turn_vectors():
            bank = back_bank("vec_bank", [P, P])
            nc.tensor.transpose(bank[:], vec_f32[:], ident[:])
            nc.vector.tensor_copy(out=cols[:], in_=bank[:, 0:24])

        def derive_columns():
            nc.vector.tensor_scalar(
                out=raised_bias_col[:], in0=bias_col, scalar1=-W_LOW, scalar2=None, op0=ALU.add
            )
            for col, weight in ((floor_col, W_LOW), (ceil_col, W_HIGH)):
                nc.vector.scalar_tensor_tensor(
                    out=col[:], in0=travel_col, scalar=weight, in1=rest_col, op0=ALU.mult, op1=ALU.add
                )
            moved = work.tile([P, 8], F32, name="moved", bufs=1)
            nc.vector.tensor_tensor(out=moved[:], in0=travel_col, in1=bias_col, op=ALU.mult)
            nc.vector.tensor_tensor(out=low_col[:], in0=floor_col[:], in1=ceil_col[:], op=ALU.min)
            nc.vector.tensor_tensor(out=high_col[:], in0=floor_col[:], in1=ceil_col[:], op=ALU.max)
            nc.vector.tensor_tensor(out=shift_col[:], in0=moved[:], in1=rest_col, op=ALU.add)

        row_banks = {}

        def turn_row(v, new_bank):
            col = (raised_bias_col[:], travel_col, floor_col[:])[v]
            if True:
                bank = new_bank("row_bank", [P, HALF])
                row_banks[v] = bank
                for b in range(BLOCKS):
                    nc.tensor.transpose(
                        bank[:, P * b : P * (b + 1)], col[:, b : b + 1].to_broadcast([P, P]), ident[:]
                    )

        def store_row(v, engine_copy):
            engine_copy(out=(raised_bias_row, travel_row, floor_row)[v][:], in_=row_banks[v][:])

        def group_solver(h, on_scalar):
            source = solver_raw[h][:].rearrange("p t (c i) -> p c t i", i=4)
            target = solver_grouped[h][:].rearrange("p (c i) t -> p c t i", i=4)
            if on_scalar:
                nc.scalar.copy(out=target, in_=source)
            else:
                nc.vector.tensor_copy(out=target, in_=source)

        def quantize_solver(h):
            nc.vector.quantize_mx(
                out=solver_codes[h][:].bitcast(FP8X4),
                scales=solver_scales[h][:],
                in_=solver_grouped[h][:].rearrange("p n t -> p (n t)"),
            )

        grouped, split = {}, {}

        def split_tile(j):
            new = work.tile([P, PASSES, 2, P], F32, name="split_tile", tag="split", bufs=SPLIT_BUFS, align_bytes=64)
            split["tile", j] = new
            nc.vector.tensor_copy(
                out=new[:], in_=tile_raw[j][:].bitcast(F32).rearrange("p (c m u) -> p c u m", c=PASSES, u=2)
            )

        def turn_tile(j):
            new = work.tile([P, PASSES, P, 4], BF16, name="grouped_tile", tag="grouped", bufs=3, align_bytes=64)
            grouped["tile", j] = new
            pairs = tile_raw[j][:].bitcast(F32)
            by_pair = new[:].rearrange("p c r t -> p (c r t)").bitcast(F32).rearrange(
                "p (c r u) -> p c r u", c=PASSES, u=2
            )
            for c0 in (0, 2):
                bank = turn_bank("tile_bank", [P, 2, 2, P])
                for c in (0, 1):
                    first = KP // 2 * (c0 + c)
                    for u in range(2):
                        source = split["tile", j][:, c0 + c, u, :] if ("tile", j) in split else pairs[:, first + u : first + KP // 2 : 2]
                        nc.tensor.transpose(bank[:, c, u, :], source, ident[:])
                nc.scalar.copy(out=by_pair[:, c0 : c0 + 2, :, :], in_=bank[:].rearrange("p c u r -> p c r u"))

        def quantize_tile(j, passes=range(PASSES)):
            frames_j = slice(P * j, P * (j + 1))
            for c in passes:
                nc.vector.quantize_mx(
                    out=codes[0][:, c, frames_j].bitcast(FP8X4),
                    scales=scales[0][:, c, frames_j],
                    in_=grouped["tile", j][:, c, :, :].rearrange("p r t -> p (r t)"),
                )

        def split_pass(n):
            new = work.tile([P, TILES, 2, P], F32, name="split", tag="split", bufs=SPLIT_BUFS, align_bytes=64)
            split[n] = new
            nc.vector.tensor_copy(
                out=new[:], in_=pass_raw[n][:].bitcast(F32).rearrange("p j (m u) -> p j u m", u=2)
            )

        def turn_pass(n):
            new = work.tile([P, TILES, P, 4], BF16, name="grouped_pass", tag="grouped", bufs=3, align_bytes=64)
            grouped["pass", n] = new
            pairs = pass_raw[n][:].bitcast(F32)
            by_pair = new[:].rearrange("p j r t -> p (j r t)").bitcast(F32).rearrange(
                "p (j r u) -> p j r u", j=TILES, u=2
            )
            for j0 in (0, 2):
                bank = turn_bank("pass_bank", [P, 2, 2, P])
                for j in (0, 1):
                    for u in range(2):
                        source = split[n][:, j0 + j, u, :] if n in split else pairs[:, j0 + j, u : KP // 2 : 2]
                        nc.tensor.transpose(bank[:, j, u, :], source, ident[:])
                nc.scalar.copy(out=by_pair[:, j0 : j0 + 2, :, :], in_=bank[:].rearrange("p j u r -> p j r u"))

        def quantize_pass(n):
            g, c = n // PASSES + 1, n % PASSES
            nc.vector.quantize_mx(
                out=codes[g][:, c, :].bitcast(FP8X4),
                scales=scales[g][:, c, :],
                in_=grouped["pass", n][:].rearrange("p j r t -> p (j r t)"),
            )

        def solver_operand(c, h, first, last):
            if c < SKIN_PASSES:
                column = N * c + HALF * h
                return words[h][:, c, 2 * first : 2 * last].bitcast(FP4X4), word_scales[:, column + first : column + last]
            return solver_codes[h][:, first:last].bitcast(FP8X4), solver_scales[h][:, first:last]

        def frame_operand(g, c, first, last):
            return codes[g][:, c, first:last].bitcast(FP8X4), scales[g][:, c, first:last]

        def multiply(acc, c, stationary, moving):
            nc.tensor.matmul_mx(
                out=acc,
                lhsT=stationary[0],
                lhsT_scale=stationary[1],
                rhs=moving[0],
                rhs_scale=moving[1],
                start=(c == 0),
                stop=(c == PASSES - 1),
            )

        f_acc, f_raised, f_relu, f_moved = {}, {}, {}, {}

        def f_product(i, passes=range(PASSES)):
            g, j = divmod(i, TILES)
            if passes[0] == 0:
                new = acc_bank("f_acc")
                f_acc[i] = new
            for c in passes:
                multiply(f_acc[i][:], c, frame_operand(g, c, P * j, P * (j + 1)), solver_operand(c, 0, 0, HALF))

        def f_add_bias(i):
            new = work.tile([P, HALF], F32, name="f_raised", align_bytes=64)
            f_raised[i] = new
            nc.vector.tensor_tensor(out=new[:], in0=f_acc[i][:], in1=raised_bias_row[:], op=ALU.add)

        def f_clamp_low(i):
            new = work.tile([P, HALF], F32, name="f_relu", align_bytes=64)
            f_relu[i] = new
            nc.scalar.activation(out=new[:], in_=f_raised[i][:], func=ACT.Relu)

        def f_clamp_high_and_scale(i):
            new = work.tile([P, HALF], F32, name="f_moved", align_bytes=64)
            f_moved[i] = new
            nc.vector.scalar_tensor_tensor(
                out=new[:], in0=f_relu[i][:], scalar=W_HIGH - W_LOW, in1=travel_row[:], op0=ALU.min, op1=ALU.mult
            )

        def f_finish(i):
            g, j = divmod(i, TILES)
            result = work.tile([P, HALF], F32, name="f_result", tag="result", bufs=6, align_bytes=64)
            nc.vector.tensor_tensor(out=result[:], in0=f_moved[i][:], in1=floor_row[:], op=ALU.add)
            nc.sync.dma_start(out=group_rows(out, g)[:, j, 0:HALF], in_=result[:])

        c_acc, c_affine, c_clamped, c_turned, c_pair = {}, {}, {}, {}, {}

        def c_column(i):
            return slice(BLOCKS + i % BLOCKS, BLOCKS + i % BLOCKS + 1)

        def c_product(i):
            g, b = divmod(i, BLOCKS)
            new = acc_bank("c_acc")
            c_acc[i] = new
            for c in range(PASSES):
                multiply(new[:], c, solver_operand(c, 1, P * b, P * (b + 1)), frame_operand(g, c, 0, GROUP))

        def c_scale_and_shift(i, acc, width):
            new = work.tile([P, width], F32, name="c_affine", align_bytes=64)
            nc.scalar.activation(
                out=new[:], in_=acc, func=ACT.Identity, bias=shift_col[:, c_column(i)], scale=travel_col[:, c_column(i)]
            )
            return new

        def c_clamp(i, affine, width):
            new = work.tile([P, width], F32, name="c_clamped", bufs=4, align_bytes=64)
            nc.vector.tensor_scalar(
                out=new[:],
                in0=affine[:],
                scalar1=low_col[:, c_column(i)],
                scalar2=high_col[:, c_column(i)],
                op0=ALU.max,
                op1=ALU.min,
            )
            return new

        def c_turn_back(clamped, tiles):
            bank = back_bank("back_bank", [P, tiles, P])
            for j in range(tiles):
                nc.tensor.transpose(bank[:, j, :], clamped[:, P * j : P * (j + 1)], ident[:])
            return bank

        def c_finish(i, bank):
            g, b = divmod(i, BLOCKS)
            if b % 2 == 0:
                new = work.tile([P, TILES, 2, P], F32, name="c_pair", align_bytes=64)
                c_pair[i // 2] = new
            pair = c_pair[i // 2]
            nc.scalar.copy(out=pair[:, :, b % 2, :], in_=bank[:])
            if b % 2 == 1:
                first = HALF + P * (b - 1)
                nc.sync.dma_start(
                    out=group_rows(out, g)[:, :, first : first + 2 * P], in_=pair[:].rearrange("p j b n -> p j (b n)")
                )

        def c_return(i):
            c_finish(i, c_turn_back(c_clamped[i], TILES))

        def c_scale(i):
            c_affine[i] = c_scale_and_shift(i, c_acc[i][:], GROUP)

        def c_limit(i):
            c_clamped[i] = c_clamp(i, c_affine[i], GROUP)

        END = UNITS - 1

        def end_store(bank, engine_copy, i, j0, tiles):
            first = HALF + P * (i % BLOCKS)
            result = work.tile([P, tiles, P], F32, name="end_result", tag="result", bufs=6, align_bytes=64)
            engine_copy(out=result[:], in_=bank[:])
            nc.sync.dma_start(out=group_rows(out, GROUPS - 1)[:, j0 : j0 + tiles, first : first + P], in_=result[:])

        def end_product(half):
            b = END % BLOCKS
            acc = turn_bank("end_acc", [P, 2, P])
            for j in range(2):
                first = P * (2 * half + j)
                for c in range(PASSES):
                    multiply(
                        acc[:, j, :],
                        c,
                        solver_operand(c, 1, P * b, P * (b + 1)),
                        frame_operand(GROUPS - 1, c, first, first + P),
                    )
            return acc[:].rearrange("p j r -> p (j r)")

        done = set()
        c_bank = {}

        def c_back(i):
            c_bank[i] = c_turn_back(c_clamped[i], TILES)

        def c_store(i):
            c_finish(i, c_bank[i])

        RANGES = {
            split_pass: (1, 12), turn_pass: (0, 12), quantize_pass: (0, 12),
            f_product: (1, 16), f_add_bias: (0, 16), f_clamp_low: (0, 16), f_clamp_high_and_scale: (0, 16), f_finish: (0, 16),
            c_product: (0, 15), c_scale: (0, 15), c_limit: (0, 15), c_back: (0, 15), c_store: (0, 14),
        }

        def once(op, n):
            if (op, n) in done or not RANGES[op][0] <= n < RANGES[op][1]:
                return
            done.add((op, n))
            op(n)

        turn_tile(0)
        warm_quant()
        quantize_tile(0, (0, 1))
        warm_up(2)
        group_solver(0, True)
        quantize_tile(0, (2, 3))
        f_product(0, range(SKIN_PASSES))
        widen_vectors()
        turn_vectors()
        derive_columns()
        turn_tile(1)
        quantize_solver(0)
        group_solver(1, False)
        quantize_tile(1, (0, 1))
        quantize_tile(1, (2, 3))
        split_tile(3)
        warm_up(4)
        turn_row(0, back_bank)
        turn_tile(2)
        f_product(0, range(SKIN_PASSES, PASSES))
        quantize_solver(1)
        once(f_product, 1)
        turn_row(1, back_bank)
        store_row(0, nc.scalar.copy)
        turn_row(2, back_bank)
        quantize_tile(2, (0, 1))
        once(f_add_bias, 0)
        once(f_add_bias, 1)
        quantize_tile(2, (2, 3))
        turn_tile(3)
        once(f_clamp_low, 1)
        quantize_tile(3, (0, 1))
        quantize_tile(3, (2, 3))
        once(f_product, 2)
        store_row(1, nc.vector.tensor_copy)
        once(f_clamp_low, 0)
        once(split_pass, 1)
        once(turn_pass, 0)
        once(split_pass, 2)
        store_row(2, nc.vector.tensor_copy)
        once(f_clamp_high_and_scale, 1)
        once(c_product, 0)
        once(f_add_bias, 2)
        once(split_pass, 3)
        once(c_scale, 0)
        once(f_clamp_low, 2)
        once(turn_pass, 1)
        once(f_product, 3)
        once(c_product, 1)
        once(f_clamp_high_and_scale, 2)
        once(c_scale, 1)
        once(f_add_bias, 3)
        once(turn_pass, 2)
        once(c_limit, 0)
        once(f_finish, 1)
        once(c_limit, 1)
        once(quantize_pass, 0)
        once(f_clamp_high_and_scale, 0)
        once(c_product, 2)
        once(c_scale, 2)
        once(turn_pass, 3)
        once(c_back, 0)
        once(quantize_pass, 1)
        once(split_pass, 4)
        once(c_back, 1)
        once(f_finish, 0)
        once(quantize_pass, 2)
        once(c_limit, 2)
        once(c_product, 3)
        once(c_store, 0)
        once(quantize_pass, 3)
        once(f_finish, 2)
        once(c_scale, 3)
        once(split_pass, 5)
        once(c_store, 1)
        for i in range(4, UNITS, 2):
            once(c_limit, i + -1)
            once(turn_pass, i + 0)
            once(f_product, i + 0)
            once(f_add_bias, i + 0)
            once(f_clamp_low, i + -1)
            once(f_clamp_low, i + 0)
            once(c_product, i + 0)
            once(c_back, i + -2)
            once(c_store, i + -2)
            once(f_clamp_high_and_scale, i + -1)
            once(split_pass, i + 2)
            once(c_back, i + -1)
            once(c_store, i + -1)
            once(f_clamp_high_and_scale, i + 0)
            once(quantize_pass, i + 0)
            once(split_pass, i + 3)
            once(turn_pass, i + 1)
            once(f_product, i + 1)
            once(quantize_pass, i + 1)
            once(c_product, i + 1)
            once(f_finish, i + -1)
            once(f_add_bias, i + 1)
            once(c_scale, i + 0)
            once(c_limit, i + 0)
            once(f_finish, i + 0)
            once(c_scale, i + 1)
        once(f_add_bias, 14)
        acc_0 = end_product(0)
        affine_0 = c_scale_and_shift(END, acc_0, GROUP // 2)
        once(f_clamp_low, 14)
        once(f_finish, 13)
        once(c_scale, 14)
        once(f_clamp_high_and_scale, 13)
        once(c_back, 13)
        acc_1 = end_product(1)
        once(f_add_bias, 13)
        once(f_clamp_low, 15)
        once(c_scale, 13)
        once(f_clamp_low, 13)
        once(f_clamp_high_and_scale, 14)
        once(c_back, 14)
        once(f_finish, 12)
        affine_1 = c_scale_and_shift(END, acc_1, GROUP // 2)
        clamped_0 = c_clamp(END, affine_0, GROUP // 2)
        once(f_clamp_high_and_scale, 15)
        back_0 = c_turn_back(clamped_0, 2)
        once(f_add_bias, 15)
        clamped_1 = c_clamp(END, affine_1, GROUP // 2)
        end_store(c_bank[14], nc.scalar.copy, END - 1, 0, TILES)
        back_1 = c_turn_back(clamped_1, 2)
        once(c_store, 13)
        once(c_back, 12)
        once(c_limit, 13)
        end_store(back_0, nc.scalar.copy, END, 0, 2)
        once(f_finish, 15)
        end_store(back_1, nc.scalar.copy, END, 2, 2)
        once(c_limit, 14)
        once(f_finish, 14)
        once(c_store, 12)
        missing = [(0, n) for op in RANGES for n in range(RANGES[op][0], RANGES[op][1]) if (op, n) not in done]
        assert not missing, missing
